import numpy as np
import ml_dtypes


def mxq(x, axis, fmt="e4m3"):
    dtype, down = {"e4m3": (ml_dtypes.float8_e4m3fn, 7), "e5m2": (ml_dtypes.float8_e5m2, 14)}[fmt]
    v = np.moveaxis(np.asarray(x, np.float32).astype(ml_dtypes.bfloat16).astype(np.float64), axis, -1)
    blocks = v.reshape(v.shape[:-1] + (-1, 32))
    amax = np.abs(blocks).max(-1, keepdims=True)
    byte = np.maximum(np.where(amax > 0, np.frexp(amax)[1] - 1 + 127, 0) - down, 1)
    scale = np.exp2(byte - 127.0)
    codes = (blocks / scale).astype(np.float32).astype(dtype).astype(np.float64)
    return np.moveaxis((codes * scale).reshape(v.shape), -1, axis)


WIDE = False


def mx_kscale(k):
    if not WIDE:
        return np.ones(k)
    levels = np.array([10, -10, 5, -5, 0])
    if k % 512:
        return np.exp2(np.random.permutation(np.resize(levels, k // 32))).repeat(32)
    a = np.empty((k // 512, 16))
    for p in range(k // 512):
        a[p, :8] = np.random.permutation(np.resize(levels, 8))
        for g in range(8):
            far = levels[np.abs(levels - a[p, g]) >= 10]
            a[p, g + 8] = far[np.random.randint(len(far))]
    return np.exp2(a.ravel()).repeat(32)


def f64(x):
    return np.asarray(x).astype(np.float64)


def striped(idx):
    return np.tile(idx.reshape(-1, 16).T, (8, 1)).astype(np.uint16)


def unstriped(offs):
    return offs[:16].T.reshape(-1).astype(np.int64)


E2M1 = np.array([0.0, 0.5, 1.0, 1.5, 2.0, 3.0, 4.0, 6.0, -0.0, -0.5, -1.0, -1.5, -2.0, -3.0, -4.0, -6.0])


def pack_weight(w, fmt):
    k, n = w.shape
    w = f64(np.asarray(w, np.float32).astype(ml_dtypes.bfloat16)).reshape(k // 32, 32, n)
    amax = np.abs(w).max(1)
    if fmt == "e4m3":
        byte = np.frexp(amax)[1] - 1 + 127 - 7
    else:
        mant, ex = np.frexp(amax / 6.0)
        byte = np.where(mant > 0.5, ex, ex - 1) + 127
    byte = np.clip(np.where(amax > 0, byte, 1), 1, 254)
    scaled = (w * np.exp2(127.0 - byte)[:, None, :]).reshape(k, n).astype(np.float32)
    by_word = np.ascontiguousarray(scaled.reshape(k // 512, 128, 4, n).transpose(0, 1, 3, 2))
    if fmt == "e4m3":
        words = by_word.astype(ml_dtypes.float8_e4m3fn).view(np.uint8)
    else:
        c = by_word.astype(ml_dtypes.float4_e2m1fn).view(np.uint8) & 0xF
        words = (c[..., 0::2] | (c[..., 1::2] << 4)).reshape(k // 512, 128, 2 * n)
    return np.ascontiguousarray(words), np.ascontiguousarray(byte.astype(np.uint8).reshape(k // 512, 16, n))


def unpack_weight(words, scales, fmt):
    g, _, n = scales.shape
    words = np.ascontiguousarray(words).reshape(g, 128, n, -1)
    if fmt == "e4m3":
        vals = words.view(ml_dtypes.float8_e4m3fn).astype(np.float64)
    else:
        nib = np.empty((g, 128, n, 4), np.uint8)
        nib[..., 0::2] = words & 0xF
        nib[..., 1::2] = words >> 4
        vals = E2M1[nib]
    vals = vals * np.repeat(np.exp2(scales.astype(np.float64) - 127.0), 8, axis=1)[..., None]
    return vals.transpose(0, 1, 3, 2).reshape(g * 512, n)


def pack_table(v):
    words, scales = pack_weight(v, "e4m3")
    return np.concatenate([words.reshape(words.shape[0], -1), scales.reshape(scales.shape[0], -1)], axis=1)


def unpack_table(tab):
    g, t = tab.shape[0], tab.shape[1] // 528
    return unpack_weight(tab[:, :512 * t].reshape(g, 128, t, 4), tab[:, 512 * t:].reshape(g, 16, t), "e4m3")


def silu(v):
    return v / (1.0 + np.exp(-np.maximum(v, -700.0)))


K, M, T, S = 1024, 256, 4096, 2048


def setup_inputs():
    n = np.random.standard_normal
    s = mx_kscale(K)[:, None]
    return {
        "tab": pack_table(n((K, T)) * s),
        "w": (n((K, M)) / np.sqrt(K) / s).astype(np.float32),
        "b": (0.3 * n(256)).astype(np.float32),
        "wgo": np.tile(np.random.uniform(0.5, 2.0, S), (128, 1)).astype(np.float32),
        "offs": striped(np.random.permutation(T)[:S]),
        "offs2": striped(np.random.permutation(T)[:S]),
    }


def reference(tab, w, b, wgo, offs, offs2):
    tab_ = unpack_table(tab)[:, unstriped(offs)]
    w_ = mxq(f64(w), 0, "e4m3")
    y = w_.T @ tab_
    out = np.zeros((M, T))
    out[:, unstriped(offs2)] = f64(wgo)[0] * (silu(y + f64(b)[:, None]))
    return out

@@ -1,0 +1,138 @@
+import concourse.mybir as mybir
+
+K, M, T, S = 1024, 256, 4096, 2048
+P = 128
+PASSES = K // 512
+M_TILES = M // P
+N_TILE = 512
+SLICES = S // N_TILE
+COLS = N_TILE // 16
+
+F32 = mybir.dt.float32
+BF16 = mybir.dt.bfloat16
+I32 = mybir.dt.int32
+U32 = mybir.dt.uint32
+U16 = mybir.dt.uint16
+U8 = mybir.dt.uint8
+FP8X4 = mybir.dt.float8_e4m3fn_x4
+MULT = mybir.AluOpType.mult
+SILU = mybir.ActivationFunctionType.Silu
+
+FLOPS = 2 * K * M * S
+
+
+def tile_list_tabscat_silu_kernel(tc, tab, w, b, wgo, offs, offs2, out):
+    nc = tc.nc
+    with tc.tile_pool(name="hold", bufs=1) as hold, tc.psum_pool(name="psum", bufs=1) as psum:
+        list_in = hold.tile([P, S // 16], U16, name="list_in")
+        list_out = hold.tile([P, S // 16], U16, name="list_out")
+        nc.sync.dma_start(list_in[:], offs)
+
+        scales = hold.tile([P, T], U8, name="scales", align_bytes=64)
+        scale_words = scales[:].bitcast(I32)
+        nc.vector.memset(scale_words, 0)
+        scale_rows = tab[:, 512 * T : 528 * T].rearrange("a (q t) -> a q t", q=16)
+        for quad in range(4):
+            rows = scale_rows[:, 4 * quad : 4 * quad + 4, :].bitcast(I32)
+            if quad < 3:
+                for a in range(PASSES):
+                    p0 = 32 * quad + 4 * a
+                    nc.sync.dma_start(scale_words[p0 : p0 + 4, :], rows[a])
+            else:
+                nc.sync.dma_start(scale_words[32 * quad : 32 * quad + 8, :], rows)
+
+        words = [hold.tile([P, T], I32, name=f"words{a}", align_bytes=64) for a in range(PASSES)]
+        w_raw = [hold.tile([P, 4, M], F32, name=f"w_raw{a}") for a in range(PASSES)]
+        word_rows = [tab[a, 0 : 512 * T].rearrange("(p x) -> p x", p=P).bitcast(I32) for a in range(PASSES)]
+        weight_out = hold.tile([P, S], F32, name="weight_out")
+        for tile in (words[0][:, 0:8], words[1][:, 0:8]):
+            nc.vector.memset(tile, 0)
+        for tile in (w_raw[0][:, 0, 0:8], w_raw[1][:, 0, 0:8], weight_out[:, 0:8]):
+            nc.vector.memset(tile, 0.0)
+        for a in range(PASSES):
+            nc.sync.dma_start(words[a][:], word_rows[a])
+        for a in range(PASSES):
+            nc.sync.dma_start(w_raw[a][:], w[512 * a : 512 * (a + 1), :].rearrange("(p j) n -> p j n", j=4))
+        bias = hold.tile([P, M_TILES], F32, name="bias")
+        nc.sync.dma_start(bias[:], b.rearrange("(m p) -> p m", p=P))
+        nc.sync.dma_start(weight_out[:], wgo)
+        nc.sync.dma_start(list_out[:], offs2)
+
+        windows = [hold.tile([P, T], F32, name=f"window{m}") for m in range(M_TILES)]
+        nc.vector.memset(windows[0][:], 0.0)
+        nc.vector.memset(windows[1][:, 0:8], 0.0)
+        nc.gpsimd.memset(windows[1][:], 0.0)
+
+        warm = hold.tile([P, 1], F32, name="warm")
+        nc.vector.memset(warm[:], 0.0)
+        warmed = hold.tile([P, 1], F32, name="warmed")
+        nc.scalar.activation(warmed[:], warm[:], SILU)
+
+        picked_scales = hold.tile([P, S], U8, name="picked_scales", align_bytes=64)
+        nc.vector.tensor_copy(picked_scales[:], scales[:].indirect(list_in[:]))
+        picked_first = hold.tile([P, S], U32, name="picked_first", align_bytes=64)
+        nc.vector.tensor_copy(picked_first[:], words[0][:].bitcast(U32).indirect(list_in[:]))
+
+        w_inter = [
+            hold.tile([P, PASSES, P, 4], BF16, name=f"w_inter{m}", tag=f"turn{m}", align_bytes=64) for m in range(M_TILES)
+        ]
+        w_codes = hold.tile([P, M_TILES, PASSES, P], U32, name="w_codes", align_bytes=64)
+        w_scales = hold.tile([P, M_TILES, PASSES, P], U8, name="w_scales", align_bytes=64)
+        for a in range(PASSES):
+            for m in range(M_TILES):
+                nc.scalar.copy(w_inter[m][:, a, :, :], w_raw[a][:, :, P * m : P * (m + 1)].rearrange("p j n -> p n j"))
+
+        def quantise(m):
+            nc.vector.quantize_mx(
+                out=w_codes[:, m, :, :].rearrange("p a n -> p (a n)").bitcast(FP8X4),
+                scales=w_scales[:, m, :, :].rearrange("p a n -> p (a n)"),
+                in_=w_inter[m][:].rearrange("p a n j -> p (a n j)"),
+            )
+
+        def gather_half(h):
+            half = hold.tile([P, S // 2], U32, name=f"picked_last{h}", tag="turn0" if h else "picked_last0", align_bytes=64)
+            cols = slice(S // 32 * h, S // 32 * (h + 1))
+            nc.vector.tensor_copy(half[:], words[1][:].bitcast(U32).indirect(list_in[:, cols]))
+            return half
+
+
+        results = [hold.tile([P, S], F32, name=f"result{m}") for m in range(M_TILES)]
+
+        def multiply(m, s):
+            cols = slice(N_TILE * s, N_TILE * (s + 1))
+            inner = slice(N_TILE * (s % 2), N_TILE * (s % 2 + 1))
+            rhs = [picked_first[:, cols], picked_last[s // 2][:, inner]]
+            acc = psum.tile([P, N_TILE], F32, name=f"acc{m}_{s}")
+            for a in range(PASSES):
+                nc.tensor.matmul_mx(
+                    out=acc[:],
+                    lhsT=w_codes[:, m, a, :].bitcast(FP8X4),
+                    lhsT_scale=w_scales[:, m, a, :],
+                    rhs=rhs[a].bitcast(FP8X4),
+                    rhs_scale=picked_scales[4 * a : P, cols],
+                    start=(a == 0),
+                    stop=(a == PASSES - 1),
+                )
+            nc.scalar.activation(results[m][:, cols], acc[:], SILU, bias=bias[:, m : m + 1])
+
+        def scatter(m, first, last):
+            cols = slice(N_TILE * first, N_TILE * last)
+            nc.vector.tensor_tensor(
+                windows[m][:].indirect(list_out[:, COLS * first : COLS * last]),
+                results[m][:, cols],
+                weight_out[:, cols],
+                MULT,
+            )
+
+        picked_last = [gather_half(0)]
+        quantise(0)
+        picked_last.append(gather_half(1))
+        quantise(1)
+        for m in range(M_TILES):
+            for s in range(SLICES):
+                multiply(m, s)
+        scatter(0, 0, 1)
+        scatter(0, 1, SLICES)
+        nc.sync.dma_start(out[0:P, :], windows[0][:])
+        scatter(1, 0, SLICES)
+        nc.sync.dma_start(out[P : 2 * P, :], windows[1][:])

@@ -58,10 +58,8 @@ def tile_list_tabscat_silu_kernel(tc, tab, w, b, wgo, offs, offs2, out):
         nc.sync.dma_start(weight_out[:], wgo)
         nc.sync.dma_start(list_out[:], offs2)
 
-        windows = [hold.tile([P, T], F32, name=f"window{m}") for m in range(M_TILES)]
+        windows = [hold.tile([P, T], F32, name="window0")]
         nc.vector.memset(windows[0][:], 0.0)
-        nc.vector.memset(windows[1][:, 0:8], 0.0)
-        nc.gpsimd.memset(windows[1][:], 0.0)
 
         warm = hold.tile([P, 1], F32, name="warm")
         nc.vector.memset(warm[:], 0.0)
@@ -70,7 +68,7 @@ def tile_list_tabscat_silu_kernel(tc, tab, w, b, wgo, offs, offs2, out):
 
         picked_scales = hold.tile([P, S], U8, name="picked_scales", align_bytes=64)
         nc.vector.tensor_copy(picked_scales[:], scales[:].indirect(list_in[:]))
-        picked_first = hold.tile([P, S], U32, name="picked_first", align_bytes=64)
+        picked_first = hold.tile([P, S], U32, name="picked_first", tag="late", align_bytes=64)
         nc.vector.tensor_copy(picked_first[:], words[0][:].bitcast(U32).indirect(list_in[:]))
 
         w_inter = [
@@ -131,6 +129,8 @@ def tile_list_tabscat_silu_kernel(tc, tab, w, b, wgo, offs, offs2, out):
         for m in range(M_TILES):
             for s in range(SLICES):
                 multiply(m, s)
+        windows.append(hold.tile([P, T], F32, name="window1", tag="late", align_bytes=64))
+        nc.gpsimd.memset(windows[1][:], 0.0)
         scatter(0, 0, 1)
         scatter(0, 1, SLICES)
         nc.sync.dma_start(out[0:P, :], windows[0][:])

@@ -28,57 +28,57 @@ def tile_list_tabscat_silu_kernel(tc, tab, w, b, wgo, offs, offs2, out):
         list_out = hold.tile([P, S // 16], U16, name="list_out")
         nc.sync.dma_start(list_in[:], offs)
 
-        scales = hold.tile([P, T], U8, name="scales", align_bytes=64)
-        scale_words = scales[:].bitcast(I32)
-        nc.vector.memset(scale_words, 0)
-        scale_rows = tab[:, 512 * T : 528 * T].rearrange("a (q t) -> a q t", q=16)
-        for quad in range(4):
-            rows = scale_rows[:, 4 * quad : 4 * quad + 4, :].bitcast(I32)
-            if quad < 3:
-                for a in range(PASSES):
-                    p0 = 32 * quad + 4 * a
-                    nc.sync.dma_start(scale_words[p0 : p0 + 4, :], rows[a])
-            else:
-                nc.sync.dma_start(scale_words[32 * quad : 32 * quad + 8, :], rows)
-
-        words = [hold.tile([P, T], I32, name=f"words{a}", align_bytes=64) for a in range(PASSES)]
-        w_raw = [hold.tile([P, 4, M], F32, name=f"w_raw{a}") for a in range(PASSES)]
-        word_rows = [tab[a, 0 : 512 * T].rearrange("(p x) -> p x", p=P).bitcast(I32) for a in range(PASSES)]
-        weight_out = hold.tile([P, S], F32, name="weight_out")
-        for tile in (words[0][:, 0:8], words[1][:, 0:8]):
-            nc.vector.memset(tile, 0)
-        for tile in (w_raw[0][:, 0, 0:8], w_raw[1][:, 0, 0:8], weight_out[:, 0:8]):
-            nc.vector.memset(tile, 0.0)
-        for a in range(PASSES):
-            nc.sync.dma_start(words[a][:], word_rows[a])
-        for a in range(PASSES):
-            nc.sync.dma_start(w_raw[a][:], w[512 * a : 512 * (a + 1), :].rearrange("(p j) n -> p j n", j=4))
-        bias = hold.tile([P, M_TILES], F32, name="bias")
-        nc.sync.dma_start(bias[:], b.rearrange("(m p) -> p m", p=P))
-        nc.sync.dma_start(weight_out[:], wgo)
-        nc.sync.dma_start(list_out[:], offs2)
-
-        windows = [hold.tile([P, T], F32, name="window0")]
-        nc.vector.memset(windows[0][:], 0.0)
-
         warm = hold.tile([P, 1], F32, name="warm")
-        nc.vector.memset(warm[:], 0.0)
+        nc.gpsimd.memset(warm[:], 0.0)
         warmed = hold.tile([P, 1], F32, name="warmed")
         nc.scalar.activation(warmed[:], warm[:], SILU)
 
+        scales = hold.tile([P, T], U8, name="scales", tag="early", align_bytes=64)
+        scale_words = scales[:].bitcast(I32)
+        nc.gpsimd.memset(scale_words[32:64, :], 0)
+        nc.gpsimd.memset(scale_words[64:P, :], 0)
+        for a in range(PASSES):
+            rows = tab[a, 512 * T : 528 * T].rearrange("(q t) -> q t", q=16).bitcast(I32)
+            nc.sync.dma_start(scale_words[16 * a : 16 * (a + 1), :], rows)
+
+        words = [hold.tile([P, T], I32, name=f"words{a}", align_bytes=64) for a in range(PASSES)]
+        for a in range(PASSES):
+            nc.sync.dma_start(words[a][:], tab[a, 0 : 512 * T].rearrange("(p x) -> p x", p=P).bitcast(I32))
+        nc.sync.dma_start(list_out[:], offs2)
+        bias = hold.tile([P, M_TILES], F32, name="bias")
+        nc.sync.dma_start(bias[:], b.rearrange("(m p) -> p m", p=P))
+
+        planes = hold.tile([P, S], U8, name="planes", align_bytes=64)
+        plane_words = planes[:].bitcast(I32)
+        nc.gpsimd.memset(plane_words, 0)
+        windows = [hold.tile([P, T], F32, name=f"window{m}") for m in range(M_TILES)]
+        for m in range(M_TILES):
+            nc.gpsimd.memset(windows[m][:], 0.0)
+
         picked_scales = hold.tile([P, S], U8, name="picked_scales", align_bytes=64)
         nc.vector.tensor_copy(picked_scales[:], scales[:].indirect(list_in[:]))
-        picked_first = hold.tile([P, S], U32, name="picked_first", tag="late", align_bytes=64)
+        picked_rows = picked_scales[:].bitcast(I32)
+        for a in range(PASSES):
+            for quad in range(4):
+                src = 16 * a + 4 * quad
+                dst = 32 * quad + 4 * a
+                nc.scalar.dma_start(plane_words[dst : dst + 4, :], picked_rows[src : src + 4, :])
+
+        w_raw = hold.tile([P, PASSES, 4, M], F32, name="w_raw", tag="early", align_bytes=64)
+        nc.sync.dma_start(w_raw[:], w.rearrange("(a p j) n -> p a j n", a=PASSES, j=4))
+
+        picked_first = hold.tile([P, S], U32, name="picked_first", align_bytes=64)
         nc.vector.tensor_copy(picked_first[:], words[0][:].bitcast(U32).indirect(list_in[:]))
+        weight_out = hold.tile([P, S], F32, name="weight_out", tag="words0", align_bytes=64)
+        nc.sync.dma_start(weight_out[:], wgo)
 
         w_inter = [
             hold.tile([P, PASSES, P, 4], BF16, name=f"w_inter{m}", tag=f"turn{m}", align_bytes=64) for m in range(M_TILES)
         ]
         w_codes = hold.tile([P, M_TILES, PASSES, P], U32, name="w_codes", align_bytes=64)
         w_scales = hold.tile([P, M_TILES, PASSES, P], U8, name="w_scales", align_bytes=64)
-        for a in range(PASSES):
-            for m in range(M_TILES):
-                nc.scalar.copy(w_inter[m][:, a, :, :], w_raw[a][:, :, P * m : P * (m + 1)].rearrange("p j n -> p n j"))
+        for m in range(M_TILES):
+            nc.scalar.copy(w_inter[m][:], w_raw[:, :, :, P * m : P * (m + 1)].rearrange("p a j n -> p a n j"))
 
         def quantise(m):
             nc.vector.quantize_mx(
@@ -87,19 +87,16 @@ def tile_list_tabscat_silu_kernel(tc, tab, w, b, wgo, offs, offs2, out):
                 in_=w_inter[m][:].rearrange("p a n j -> p (a n j)"),
             )
 
-        def gather_half(h):
-            half = hold.tile([P, S // 2], U32, name=f"picked_last{h}", tag="turn0" if h else "picked_last0", align_bytes=64)
-            cols = slice(S // 32 * h, S // 32 * (h + 1))
-            nc.vector.tensor_copy(half[:], words[1][:].bitcast(U32).indirect(list_in[:, cols]))
-            return half
-
+        def gather_last(first, last, tag):
+            part = hold.tile([P, N_TILE * (last - first)], U32, name=f"picked_last{first}", tag=tag, align_bytes=64)
+            nc.vector.tensor_copy(part[:], words[1][:].bitcast(U32).indirect(list_in[:, COLS * first : COLS * last]))
+            return [part[:, N_TILE * i : N_TILE * (i + 1)] for i in range(last - first)]
 
         results = [hold.tile([P, S], F32, name=f"result{m}") for m in range(M_TILES)]
 
         def multiply(m, s):
             cols = slice(N_TILE * s, N_TILE * (s + 1))
-            inner = slice(N_TILE * (s % 2), N_TILE * (s % 2 + 1))
-            rhs = [picked_first[:, cols], picked_last[s // 2][:, inner]]
+            rhs = [picked_first[:, cols], picked_last[s]]
             acc = psum.tile([P, N_TILE], F32, name=f"acc{m}_{s}")
             for a in range(PASSES):
                 nc.tensor.matmul_mx(
@@ -107,7 +104,7 @@ def tile_list_tabscat_silu_kernel(tc, tab, w, b, wgo, offs, offs2, out):
                     lhsT=w_codes[:, m, a, :].bitcast(FP8X4),
                     lhsT_scale=w_scales[:, m, a, :],
                     rhs=rhs[a].bitcast(FP8X4),
-                    rhs_scale=picked_scales[4 * a : P, cols],
+                    rhs_scale=planes[4 * a : P, cols],
                     start=(a == 0),
                     stop=(a == PASSES - 1),
                 )
@@ -122,15 +119,13 @@ def tile_list_tabscat_silu_kernel(tc, tab, w, b, wgo, offs, offs2, out):
                 MULT,
             )
 
-        picked_last = [gather_half(0)]
+        picked_last = gather_last(0, SLICES - 1, "picked_most")
         quantise(0)
-        picked_last.append(gather_half(1))
+        picked_last = picked_last + gather_last(SLICES - 1, SLICES, "turn0")
         quantise(1)
         for m in range(M_TILES):
             for s in range(SLICES):
                 multiply(m, s)
-        windows.append(hold.tile([P, T], F32, name="window1", tag="late", align_bytes=64))
-        nc.gpsimd.memset(windows[1][:], 0.0)
         scatter(0, 0, 1)
         scatter(0, 1, SLICES)
         nc.sync.dma_start(out[0:P, :], windows[0][:])

@@ -23,7 +23,11 @@ FLOPS = 2 * K * M * S
 
 def tile_list_tabscat_silu_kernel(tc, tab, w, b, wgo, offs, offs2, out):
     nc = tc.nc
-    with tc.tile_pool(name="hold", bufs=1) as hold, tc.psum_pool(name="psum", bufs=1) as psum:
+    with (
+        tc.tile_pool(name="hold", bufs=1) as hold,
+        tc.tile_pool(name="reused", bufs=1) as reused,
+        tc.psum_pool(name="psum", bufs=1) as psum,
+    ):
         list_in = hold.tile([P, S // 16], U16, name="list_in")
         list_out = hold.tile([P, S // 16], U16, name="list_out")
         nc.sync.dma_start(list_in[:], offs)
@@ -33,7 +37,7 @@ def tile_list_tabscat_silu_kernel(tc, tab, w, b, wgo, offs, offs2, out):
         warmed = hold.tile([P, 1], F32, name="warmed")
         nc.scalar.activation(warmed[:], warm[:], SILU)
 
-        scales = hold.tile([P, T], U8, name="scales", tag="early", align_bytes=64)
+        scales = reused.tile([P, T], U8, name="scales", offset=2048, align_bytes=64)
         scale_words = scales[:].bitcast(I32)
         nc.gpsimd.memset(scale_words[32:64, :], 0)
         nc.gpsimd.memset(scale_words[64:P, :], 0)
@@ -41,12 +45,13 @@ def tile_list_tabscat_silu_kernel(tc, tab, w, b, wgo, offs, offs2, out):
             rows = tab[a, 512 * T : 528 * T].rearrange("(q t) -> q t", q=16).bitcast(I32)
             nc.sync.dma_start(scale_words[16 * a : 16 * (a + 1), :], rows)
 
-        words = [hold.tile([P, T], I32, name=f"words{a}", align_bytes=64) for a in range(PASSES)]
+        words = [
+            reused.tile([P, T], I32, name="words0", offset=8192, align_bytes=64),
+            hold.tile([P, T], I32, name="words1", align_bytes=64),
+        ]
         for a in range(PASSES):
             nc.sync.dma_start(words[a][:], tab[a, 0 : 512 * T].rearrange("(p x) -> p x", p=P).bitcast(I32))
         nc.sync.dma_start(list_out[:], offs2)
-        bias = hold.tile([P, M_TILES], F32, name="bias")
-        nc.sync.dma_start(bias[:], b.rearrange("(m p) -> p m", p=P))
 
         planes = hold.tile([P, S], U8, name="planes", align_bytes=64)
         plane_words = planes[:].bitcast(I32)
@@ -58,18 +63,25 @@ def tile_list_tabscat_silu_kernel(tc, tab, w, b, wgo, offs, offs2, out):
         picked_scales = hold.tile([P, S], U8, name="picked_scales", align_bytes=64)
         nc.vector.tensor_copy(picked_scales[:], scales[:].indirect(list_in[:]))
         picked_rows = picked_scales[:].bitcast(I32)
-        for a in range(PASSES):
+
+        def carry(a):
             for quad in range(4):
                 src = 16 * a + 4 * quad
                 dst = 32 * quad + 4 * a
-                nc.scalar.dma_start(plane_words[dst : dst + 4, :], picked_rows[src : src + 4, :])
+                nc.sync.dma_start(plane_words[dst : dst + 4, :], picked_rows[src : src + 4, :])
 
-        w_raw = hold.tile([P, PASSES, 4, M], F32, name="w_raw", tag="early", align_bytes=64)
-        nc.sync.dma_start(w_raw[:], w.rearrange("(a p j) n -> p a j n", a=PASSES, j=4))
+        carry(0)
+
+        w_raw = [reused.tile([P, 4, M], F32, name=f"w_raw{a}", offset=4096 * a, align_bytes=64) for a in range(PASSES)]
+        for a in range(PASSES):
+            nc.sync.dma_start(w_raw[a][:], w[512 * a : 512 * (a + 1), :].rearrange("(p j) n -> p j n", j=4))
+        carry(1)
 
         picked_first = hold.tile([P, S], U32, name="picked_first", align_bytes=64)
         nc.vector.tensor_copy(picked_first[:], words[0][:].bitcast(U32).indirect(list_in[:]))
-        weight_out = hold.tile([P, S], F32, name="weight_out", tag="words0", align_bytes=64)
+        bias = reused.tile([P, M_TILES], F32, name="bias", offset=8192, align_bytes=64)
+        nc.sync.dma_start(bias[:], b.rearrange("(m p) -> p m", p=P))
+        weight_out = reused.tile([P, S], F32, name="weight_out", offset=16384, align_bytes=64)
         nc.sync.dma_start(weight_out[:], wgo)
 
         w_inter = [
@@ -77,8 +89,9 @@ def tile_list_tabscat_silu_kernel(tc, tab, w, b, wgo, offs, offs2, out):
         ]
         w_codes = hold.tile([P, M_TILES, PASSES, P], U32, name="w_codes", align_bytes=64)
         w_scales = hold.tile([P, M_TILES, PASSES, P], U8, name="w_scales", align_bytes=64)
-        for m in range(M_TILES):
-            nc.scalar.copy(w_inter[m][:], w_raw[:, :, :, P * m : P * (m + 1)].rearrange("p a j n -> p a n j"))
+        for a in range(PASSES):
+            for m in range(M_TILES):
+                nc.scalar.copy(w_inter[m][:, a, :, :], w_raw[a][:, :, P * m : P * (m + 1)].rearrange("p j n -> p n j"))
 
         def quantise(m):
             nc.vector.quantize_mx(
@@ -119,9 +132,9 @@ def tile_list_tabscat_silu_kernel(tc, tab, w, b, wgo, offs, offs2, out):
                 MULT,
             )
 
-        picked_last = gather_last(0, SLICES - 1, "picked_most")
+        picked_last = gather_last(0, SLICES // 2, "picked_half")
         quantise(0)
-        picked_last = picked_last + gather_last(SLICES - 1, SLICES, "turn0")
+        picked_last = picked_last + gather_last(SLICES // 2, SLICES, "turn0")
         quantise(1)
         for m in range(M_TILES):
             for s in range(SLICES):

@@ -23,37 +23,27 @@ FLOPS = 2 * K * M * S
 
 def tile_list_tabscat_silu_kernel(tc, tab, w, b, wgo, offs, offs2, out):
     nc = tc.nc
-    with (
-        tc.tile_pool(name="hold", bufs=1) as hold,
-        tc.tile_pool(name="reused", bufs=1) as reused,
-        tc.psum_pool(name="psum", bufs=1) as psum,
-    ):
+    with tc.tile_pool(name="hold", bufs=1) as hold, tc.psum_pool(name="psum", bufs=1) as psum:
         list_in = hold.tile([P, S // 16], U16, name="list_in")
         list_out = hold.tile([P, S // 16], U16, name="list_out")
         nc.sync.dma_start(list_in[:], offs)
 
-        warm = hold.tile([P, 1], F32, name="warm")
-        nc.gpsimd.memset(warm[:], 0.0)
-        warmed = hold.tile([P, 1], F32, name="warmed")
-        nc.scalar.activation(warmed[:], warm[:], SILU)
-
-        scales = reused.tile([P, T], U8, name="scales", offset=2048, align_bytes=64)
+        scales = hold.tile([P, T], U8, name="scales", align_bytes=64)
         scale_words = scales[:].bitcast(I32)
-        nc.gpsimd.memset(scale_words[32:64, :], 0)
-        nc.gpsimd.memset(scale_words[64:P, :], 0)
-        for a in range(PASSES):
-            rows = tab[a, 512 * T : 528 * T].rearrange("(q t) -> q t", q=16).bitcast(I32)
-            nc.sync.dma_start(scale_words[16 * a : 16 * (a + 1), :], rows)
+        nc.gpsimd.memset(scale_words[0:96, :], 0)
+        nc.sync.dma_start(scale_words[96:P, :], tab[:, 512 * T : 528 * T].rearrange("a (q t) -> q a t", q=16).bitcast(I32))
 
-        words = [
-            reused.tile([P, T], I32, name="words0", offset=8192, align_bytes=64),
-            hold.tile([P, T], I32, name="words1", align_bytes=64),
-        ]
+        words = [hold.tile([P, T], I32, name=f"words{a}", align_bytes=64) for a in range(PASSES)]
         for a in range(PASSES):
             nc.sync.dma_start(words[a][:], tab[a, 0 : 512 * T].rearrange("(p x) -> p x", p=P).bitcast(I32))
+        w_raw = [hold.tile([P, 4, M], F32, name=f"w_raw{a}") for a in range(PASSES)]
+        for a in range(PASSES):
+            nc.sync.dma_start(w_raw[a][:], w[512 * a : 512 * (a + 1), :].rearrange("(p j) n -> p j n", j=4))
         nc.sync.dma_start(list_out[:], offs2)
+        bias = hold.tile([P, M_TILES], F32, name="bias")
+        nc.sync.dma_start(bias[:], b.rearrange("(m p) -> p m", p=P))
 
-        planes = hold.tile([P, S], U8, name="planes", align_bytes=64)
+        planes = hold.tile([P, PASSES * S], U8, name="planes", align_bytes=64)
         plane_words = planes[:].bitcast(I32)
         nc.gpsimd.memset(plane_words, 0)
         windows = [hold.tile([P, T], F32, name=f"window{m}") for m in range(M_TILES)]
@@ -63,25 +53,12 @@ def tile_list_tabscat_silu_kernel(tc, tab, w, b, wgo, offs, offs2, out):
         picked_scales = hold.tile([P, S], U8, name="picked_scales", align_bytes=64)
         nc.vector.tensor_copy(picked_scales[:], scales[:].indirect(list_in[:]))
         picked_rows = picked_scales[:].bitcast(I32)
-
-        def carry(a):
-            for quad in range(4):
-                src = 16 * a + 4 * quad
-                dst = 32 * quad + 4 * a
-                nc.sync.dma_start(plane_words[dst : dst + 4, :], picked_rows[src : src + 4, :])
-
-        carry(0)
-
-        w_raw = [reused.tile([P, 4, M], F32, name=f"w_raw{a}", offset=4096 * a, align_bytes=64) for a in range(PASSES)]
-        for a in range(PASSES):
-            nc.sync.dma_start(w_raw[a][:], w[512 * a : 512 * (a + 1), :].rearrange("(p j) n -> p j n", j=4))
-        carry(1)
+        for quad in range(4):
+            nc.sync.dma_start(plane_words[32 * quad : 32 * quad + 4, :], picked_rows[96 + 8 * quad : 96 + 8 * quad + 8, :])
 
         picked_first = hold.tile([P, S], U32, name="picked_first", align_bytes=64)
         nc.vector.tensor_copy(picked_first[:], words[0][:].bitcast(U32).indirect(list_in[:]))
-        bias = reused.tile([P, M_TILES], F32, name="bias", offset=8192, align_bytes=64)
-        nc.sync.dma_start(bias[:], b.rearrange("(m p) -> p m", p=P))
-        weight_out = reused.tile([P, S], F32, name="weight_out", offset=16384, align_bytes=64)
+        weight_out = hold.tile([P, S], F32, name="weight_out", tag="words0", align_bytes=64)
         nc.sync.dma_start(weight_out[:], wgo)
 
         w_inter = [
@@ -117,7 +94,7 @@ def tile_list_tabscat_silu_kernel(tc, tab, w, b, wgo, offs, offs2, out):
                     lhsT=w_codes[:, m, a, :].bitcast(FP8X4),
                     lhsT_scale=w_scales[:, m, a, :],
                     rhs=rhs[a].bitcast(FP8X4),
-                    rhs_scale=planes[4 * a : P, cols],
+                    rhs_scale=planes[:, S * a + N_TILE * s : S * a + N_TILE * (s + 1)],
                     start=(a == 0),
                     stop=(a == PASSES - 1),
                 )

@@ -114,10 +114,12 @@ def tile_list_tabscat_silu_kernel(tc, tab, w, b, wgo, offs, offs2, out):
         picked_last = picked_last + gather_last(SLICES // 2, SLICES, "turn0")
         quantise(1)
         for m in range(M_TILES):
-            for s in range(SLICES):
+            multiply(m, 0)
+        for m in range(M_TILES):
+            for s in range(1, SLICES):
                 multiply(m, s)
-        scatter(0, 0, 1)
-        scatter(0, 1, SLICES)
-        nc.sync.dma_start(out[0:P, :], windows[0][:])
-        scatter(1, 0, SLICES)
-        nc.sync.dma_start(out[P : 2 * P, :], windows[1][:])
+        for m in range(M_TILES):
+            scatter(m, 0, 1)
+        for m in range(M_TILES):
+            scatter(m, 1, SLICES)
+            nc.sync.dma_start(out[P * m : P * (m + 1), :], windows[m][:])

@@ -26,12 +26,12 @@ def tile_list_tabscat_silu_kernel(tc, tab, w, b, wgo, offs, offs2, out):
     with tc.tile_pool(name="hold", bufs=1) as hold, tc.psum_pool(name="psum", bufs=1) as psum:
         list_in = hold.tile([P, S // 16], U16, name="list_in")
         list_out = hold.tile([P, S // 16], U16, name="list_out")
-        nc.sync.dma_start(list_in[:], offs)
 
         scales = hold.tile([P, T], U8, name="scales", align_bytes=64)
         scale_words = scales[:].bitcast(I32)
         nc.gpsimd.memset(scale_words[0:96, :], 0)
         nc.sync.dma_start(scale_words[96:P, :], tab[:, 512 * T : 528 * T].rearrange("a (q t) -> q a t", q=16).bitcast(I32))
+        nc.sync.dma_start(list_in[:], offs)
 
         words = [hold.tile([P, T], I32, name=f"words{a}", align_bytes=64) for a in range(PASSES)]
         for a in range(PASSES):
@@ -84,17 +84,17 @@ def tile_list_tabscat_silu_kernel(tc, tab, w, b, wgo, offs, offs2, out):
 
         results = [hold.tile([P, S], F32, name=f"result{m}") for m in range(M_TILES)]
 
-        def multiply(m, s):
-            cols = slice(N_TILE * s, N_TILE * (s + 1))
-            rhs = [picked_first[:, cols], picked_last[s]]
-            acc = psum.tile([P, N_TILE], F32, name=f"acc{m}_{s}")
+        def multiply(m, s, first=0, last=N_TILE, bank=None):
+            cols = slice(N_TILE * s + first, N_TILE * s + last)
+            rhs = [picked_first[:, cols], picked_last[s][:, first:last]]
+            acc = psum.tile([P, last - first], F32, name=f"acc{m}_{s}_{first}", tag=bank or f"bank{m}_{s}")
             for a in range(PASSES):
                 nc.tensor.matmul_mx(
                     out=acc[:],
                     lhsT=w_codes[:, m, a, :].bitcast(FP8X4),
                     lhsT_scale=w_scales[:, m, a, :],
                     rhs=rhs[a].bitcast(FP8X4),
-                    rhs_scale=planes[:, S * a + N_TILE * s : S * a + N_TILE * (s + 1)],
+                    rhs_scale=planes[:, S * a + cols.start : S * a + cols.stop],
                     start=(a == 0),
                     stop=(a == PASSES - 1),
                 )
@@ -113,8 +113,9 @@ def tile_list_tabscat_silu_kernel(tc, tab, w, b, wgo, offs, offs2, out):
         quantise(0)
         picked_last = picked_last + gather_last(SLICES // 2, SLICES, "turn0")
         quantise(1)
-        for m in range(M_TILES):
-            multiply(m, 0)
+        multiply(0, 0, 0, N_TILE // 2)
+        multiply(0, 0, N_TILE // 2, N_TILE, "bank1_3")
+        multiply(1, 0)
         for m in range(M_TILES):
             for s in range(1, SLICES):
                 multiply(m, s)

@@ -40,8 +40,10 @@ def tile_list_tabscat_silu_kernel(tc, tab, w, b, wgo, offs, offs2, out):
         for a in range(PASSES):
             nc.sync.dma_start(w_raw[a][:], w[512 * a : 512 * (a + 1), :].rearrange("(p j) n -> p j n", j=4))
         nc.sync.dma_start(list_out[:], offs2)
-        bias = hold.tile([P, M_TILES], F32, name="bias")
-        nc.sync.dma_start(bias[:], b.rearrange("(m p) -> p m", p=P))
+
+        warm = hold.tile([P, 2], F32, name="warm")
+        nc.gpsimd.memset(warm[:, 0:1], 0.0)
+        nc.scalar.activation(warm[:, 1:2], warm[:, 0:1], SILU)
 
         planes = hold.tile([P, PASSES * S], U8, name="planes", align_bytes=64)
         plane_words = planes[:].bitcast(I32)
@@ -55,11 +57,15 @@ def tile_list_tabscat_silu_kernel(tc, tab, w, b, wgo, offs, offs2, out):
         picked_rows = picked_scales[:].bitcast(I32)
         for quad in range(4):
             nc.sync.dma_start(plane_words[32 * quad : 32 * quad + 4, :], picked_rows[96 + 8 * quad : 96 + 8 * quad + 8, :])
+        late = hold.tile([P, N_TILE + 8], F32, name="late", tag="scales", align_bytes=64)
+        bias = late[:, N_TILE : N_TILE + M_TILES]
+        nc.sync.dma_start(bias, b.rearrange("(m p) -> p m", p=P))
+        nc.sync.dma_start(late[:, 0:N_TILE], wgo[:, 0:N_TILE])
 
         picked_first = hold.tile([P, S], U32, name="picked_first", align_bytes=64)
         nc.vector.tensor_copy(picked_first[:], words[0][:].bitcast(U32).indirect(list_in[:]))
-        weight_out = hold.tile([P, S], F32, name="weight_out", tag="words0", align_bytes=64)
-        nc.sync.dma_start(weight_out[:], wgo)
+        weight_rest = hold.tile([P, S - N_TILE], F32, name="weight_rest", tag="words0", align_bytes=64)
+        nc.sync.dma_start(weight_rest[:], wgo[:, N_TILE:S])
 
         w_inter = [
             hold.tile([P, PASSES, P, 4], BF16, name=f"w_inter{m}", tag=f"turn{m}", align_bytes=64) for m in range(M_TILES)
@@ -105,7 +111,7 @@ def tile_list_tabscat_silu_kernel(tc, tab, w, b, wgo, offs, offs2, out):
             nc.vector.tensor_tensor(
                 windows[m][:].indirect(list_out[:, COLS * first : COLS * last]),
                 results[m][:, cols],
-                weight_out[:, cols],
+                late[:, 0:N_TILE] if first == 0 else weight_rest[:],
                 MULT,
             )
 

@@ -36,18 +36,22 @@ def tile_list_tabscat_silu_kernel(tc, tab, w, b, wgo, offs, offs2, out):
         words = [hold.tile([P, T], I32, name=f"words{a}", align_bytes=64) for a in range(PASSES)]
         for a in range(PASSES):
             nc.sync.dma_start(words[a][:], tab[a, 0 : 512 * T].rearrange("(p x) -> p x", p=P).bitcast(I32))
-        w_raw = [hold.tile([P, 4, M], F32, name=f"w_raw{a}") for a in range(PASSES)]
-        for a in range(PASSES):
-            nc.sync.dma_start(w_raw[a][:], w[512 * a : 512 * (a + 1), :].rearrange("(p j) n -> p j n", j=4))
+        w_first = hold.tile([P, 4, M], F32, name="w_first")
+        nc.sync.dma_start(w_first[:], w[0:512, :].rearrange("(p j) n -> p j n", j=4))
+        w_last = [hold.tile([P, 4, P], F32, name=f"w_last{m}", tag=f"w_last{m}", align_bytes=64) for m in range(M_TILES)]
+        for m in range(M_TILES):
+            nc.sync.dma_start(w_last[m][:], w[512:K, P * m : P * (m + 1)].rearrange("(p j) n -> p j n", j=4))
+        w_raw = [[w_first[:, :, P * m : P * (m + 1)] for m in range(M_TILES)], [w_last[m][:] for m in range(M_TILES)]]
         nc.sync.dma_start(list_out[:], offs2)
 
         warm = hold.tile([P, 2], F32, name="warm")
         nc.gpsimd.memset(warm[:, 0:1], 0.0)
         nc.scalar.activation(warm[:, 1:2], warm[:, 0:1], SILU)
 
-        planes = hold.tile([P, PASSES * S], U8, name="planes", align_bytes=64)
-        plane_words = planes[:].bitcast(I32)
-        nc.gpsimd.memset(plane_words, 0)
+        widths = [N_TILE, S - N_TILE]
+        planes = [hold.tile([P, PASSES * width], U8, name=f"planes{i}", align_bytes=64) for i, width in enumerate(widths)]
+        for plane in planes:
+            nc.gpsimd.memset(plane[:].bitcast(I32), 0)
         windows = [hold.tile([P, T], F32, name=f"window{m}") for m in range(M_TILES)]
         for m in range(M_TILES):
             nc.gpsimd.memset(windows[m][:], 0.0)
@@ -55,12 +59,20 @@ def tile_list_tabscat_silu_kernel(tc, tab, w, b, wgo, offs, offs2, out):
         picked_scales = hold.tile([P, S], U8, name="picked_scales", align_bytes=64)
         nc.vector.tensor_copy(picked_scales[:], scales[:].indirect(list_in[:]))
         picked_rows = picked_scales[:].bitcast(I32)
-        for quad in range(4):
-            nc.sync.dma_start(plane_words[32 * quad : 32 * quad + 4, :], picked_rows[96 + 8 * quad : 96 + 8 * quad + 8, :])
+
+        def carry(part, first, last):
+            for quad in range(4):
+                nc.sync.dma_start(
+                    planes[part][:].bitcast(I32)[32 * quad : 32 * quad + 4, :],
+                    picked_rows[96 + 8 * quad : 96 + 8 * quad + 8, first // 4 : last // 4],
+                )
+
+        carry(0, 0, N_TILE)
         late = hold.tile([P, N_TILE + 8], F32, name="late", tag="scales", align_bytes=64)
         bias = late[:, N_TILE : N_TILE + M_TILES]
         nc.sync.dma_start(bias, b.rearrange("(m p) -> p m", p=P))
         nc.sync.dma_start(late[:, 0:N_TILE], wgo[:, 0:N_TILE])
+        carry(1, N_TILE, S)
 
         picked_first = hold.tile([P, S], U32, name="picked_first", align_bytes=64)
         nc.vector.tensor_copy(picked_first[:], words[0][:].bitcast(U32).indirect(list_in[:]))
@@ -74,7 +86,10 @@ def tile_list_tabscat_silu_kernel(tc, tab, w, b, wgo, offs, offs2, out):
         w_scales = hold.tile([P, M_TILES, PASSES, P], U8, name="w_scales", align_bytes=64)
         for a in range(PASSES):
             for m in range(M_TILES):
-                nc.scalar.copy(w_inter[m][:, a, :, :], w_raw[a][:, :, P * m : P * (m + 1)].rearrange("p j n -> p n j"))
+                nc.scalar.copy(
+                    w_inter[m][:, a, :, :].rearrange("p (c i) j -> p c j i", i=4),
+                    w_raw[a][m].rearrange("p j (c i) -> p c j i", i=4),
+                )
 
         def quantise(m):
             nc.vector.quantize_mx(
@@ -94,13 +109,15 @@ def tile_list_tabscat_silu_kernel(tc, tab, w, b, wgo, offs, offs2, out):
             cols = slice(N_TILE * s + first, N_TILE * s + last)
             rhs = [picked_first[:, cols], picked_last[s][:, first:last]]
             acc = psum.tile([P, last - first], F32, name=f"acc{m}_{s}_{first}", tag=bank or f"bank{m}_{s}")
+            part = min(s, 1)
             for a in range(PASSES):
+                at = widths[part] * a - N_TILE * part
                 nc.tensor.matmul_mx(
                     out=acc[:],
                     lhsT=w_codes[:, m, a, :].bitcast(FP8X4),
                     lhsT_scale=w_scales[:, m, a, :],
                     rhs=rhs[a].bitcast(FP8X4),
-                    rhs_scale=planes[:, S * a + cols.start : S * a + cols.stop],
+                    rhs_scale=planes[part][:, at + cols.start : at + cols.stop],
                     start=(a == 0),
                     stop=(a == PASSES - 1),
                 )
@@ -117,7 +134,7 @@ def tile_list_tabscat_silu_kernel(tc, tab, w, b, wgo, offs, offs2, out):
 
         picked_last = gather_last(0, SLICES // 2, "picked_half")
         quantise(0)
-        picked_last = picked_last + gather_last(SLICES // 2, SLICES, "turn0")
+        picked_last = picked_last + gather_last(SLICES // 2, SLICES, "w_last0")
         quantise(1)
         multiply(0, 0, 0, N_TILE // 2)
         multiply(0, 0, N_TILE // 2, N_TILE, "bank1_3")

@@ -7,6 +7,7 @@ M_TILES = M // P
 N_TILE = 512
 SLICES = S // N_TILE
 COLS = N_TILE // 16
+CUT = 1280
 
 F32 = mybir.dt.float32
 BF16 = mybir.dt.bfloat16
@@ -99,29 +100,30 @@ def tile_list_tabscat_silu_kernel(tc, tab, w, b, wgo, offs, offs2, out):
             )
 
         def gather_last(first, last, tag):
-            part = hold.tile([P, N_TILE * (last - first)], U32, name=f"picked_last{first}", tag=tag, align_bytes=64)
-            nc.vector.tensor_copy(part[:], words[1][:].bitcast(U32).indirect(list_in[:, COLS * first : COLS * last]))
-            return [part[:, N_TILE * i : N_TILE * (i + 1)] for i in range(last - first)]
+            part = hold.tile([P, last - first], U32, name=f"picked_last{first}", tag=tag, align_bytes=64)
+            nc.vector.tensor_copy(part[:], words[1][:].bitcast(U32).indirect(list_in[:, first // 16 : last // 16]))
+            return part
 
         results = [hold.tile([P, S], F32, name=f"result{m}") for m in range(M_TILES)]
 
-        def multiply(m, s, first=0, last=N_TILE, bank=None):
-            cols = slice(N_TILE * s + first, N_TILE * s + last)
-            rhs = [picked_first[:, cols], picked_last[s][:, first:last]]
-            acc = psum.tile([P, last - first], F32, name=f"acc{m}_{s}_{first}", tag=bank or f"bank{m}_{s}")
-            part = min(s, 1)
-            for a in range(PASSES):
-                at = widths[part] * a - N_TILE * part
-                nc.tensor.matmul_mx(
-                    out=acc[:],
-                    lhsT=w_codes[:, m, a, :].bitcast(FP8X4),
-                    lhsT_scale=w_scales[:, m, a, :],
-                    rhs=rhs[a].bitcast(FP8X4),
-                    rhs_scale=planes[part][:, at + cols.start : at + cols.stop],
-                    start=(a == 0),
-                    stop=(a == PASSES - 1),
-                )
-            nc.scalar.activation(results[m][:, cols], acc[:], SILU, bias=bias[:, m : m + 1])
+        def multiply(m, first, last, bank):
+            acc = psum.tile([P, last - first], F32, name=f"acc{m}_{first}", tag=bank)
+            part = 0 if first < N_TILE else 1
+            edges = [first] + ([CUT] if first < CUT < last else []) + [last]
+            for lo, hi in zip(edges, edges[1:]):
+                rhs = [picked_first[:, lo:hi], picked_early[:, lo:hi] if lo < CUT else picked_late[:, lo - CUT : hi - CUT]]
+                for a in range(PASSES):
+                    at = widths[part] * a - N_TILE * part
+                    nc.tensor.matmul_mx(
+                        out=acc[:, lo - first : hi - first],
+                        lhsT=w_codes[:, m, a, :].bitcast(FP8X4),
+                        lhsT_scale=w_scales[:, m, a, :],
+                        rhs=rhs[a].bitcast(FP8X4),
+                        rhs_scale=planes[part][:, at + lo : at + hi],
+                        start=(a == 0),
+                        stop=(a == PASSES - 1),
+                    )
+            nc.scalar.activation(results[m][:, first:last], acc[:], SILU, bias=bias[:, m : m + 1])
 
         def scatter(m, first, last):
             cols = slice(N_TILE * first, N_TILE * last)
@@ -132,16 +134,16 @@ def tile_list_tabscat_silu_kernel(tc, tab, w, b, wgo, offs, offs2, out):
                 MULT,
             )
 
-        picked_last = gather_last(0, SLICES // 2, "picked_half")
+        picked_early = gather_last(0, CUT, "picked_early")
         quantise(0)
-        picked_last = picked_last + gather_last(SLICES // 2, SLICES, "w_last0")
+        picked_late = gather_last(CUT, S, "w_last0")
         quantise(1)
-        multiply(0, 0, 0, N_TILE // 2)
-        multiply(0, 0, N_TILE // 2, N_TILE, "bank1_3")
-        multiply(1, 0)
+        multiply(0, 0, N_TILE // 2, "bank0_0")
+        multiply(0, N_TILE // 2, N_TILE, "bank1_3")
+        multiply(1, 0, N_TILE, "bank1_0")
         for m in range(M_TILES):
             for s in range(1, SLICES):
-                multiply(m, s)
+                multiply(m, N_TILE * s, N_TILE * (s + 1), f"bank{m}_{s}")
         for m in range(M_TILES):
             scatter(m, 0, 1)
         for m in range(M_TILES):

@@ -7,7 +7,7 @@ M_TILES = M // P
 N_TILE = 512
 SLICES = S // N_TILE
 COLS = N_TILE // 16
-CUT = 1280
+CUT = 768
 
 F32 = mybir.dt.float32
 BF16 = mybir.dt.bfloat16

@@ -7,7 +7,7 @@ M_TILES = M // P
 N_TILE = 512
 SLICES = S // N_TILE
 COLS = N_TILE // 16
-CUT = 768
+CUT = 896
 
 F32 = mybir.dt.float32
 BF16 = mybir.dt.bfloat16
@@ -37,12 +37,12 @@ def tile_list_tabscat_silu_kernel(tc, tab, w, b, wgo, offs, offs2, out):
         words = [hold.tile([P, T], I32, name=f"words{a}", align_bytes=64) for a in range(PASSES)]
         for a in range(PASSES):
             nc.sync.dma_start(words[a][:], tab[a, 0 : 512 * T].rearrange("(p x) -> p x", p=P).bitcast(I32))
-        w_first = hold.tile([P, 4, M], F32, name="w_first")
-        nc.sync.dma_start(w_first[:], w[0:512, :].rearrange("(p j) n -> p j n", j=4))
-        w_last = [hold.tile([P, 4, P], F32, name=f"w_last{m}", tag=f"w_last{m}", align_bytes=64) for m in range(M_TILES)]
-        for m in range(M_TILES):
-            nc.sync.dma_start(w_last[m][:], w[512:K, P * m : P * (m + 1)].rearrange("(p j) n -> p j n", j=4))
-        w_raw = [[w_first[:, :, P * m : P * (m + 1)] for m in range(M_TILES)], [w_last[m][:] for m in range(M_TILES)]]
+        def load_w(tile, a, m):
+            nc.sync.dma_start(tile, w[512 * a : 512 * (a + 1), P * m : P * (m + 1)].rearrange("(p j) n -> p j n", j=4))
+
+        w_early = [hold.tile([P, 4, P], F32, name=f"w_early{a}", tag=f"w_early{a}", align_bytes=64) for a in range(PASSES)]
+        for a in range(PASSES):
+            load_w(w_early[a][:], a, 0)
         nc.sync.dma_start(list_out[:], offs2)
 
         warm = hold.tile([P, 2], F32, name="warm")
@@ -69,24 +69,27 @@ def tile_list_tabscat_silu_kernel(tc, tab, w, b, wgo, offs, offs2, out):
                 )
 
         carry(0, 0, N_TILE)
-        late = hold.tile([P, N_TILE + 8], F32, name="late", tag="scales", align_bytes=64)
-        bias = late[:, N_TILE : N_TILE + M_TILES]
+        late = hold.tile([P, S + M * 4 + 8], F32, name="late", tag="scales", align_bytes=64)
+        bias = late[:, S + M * 4 : S + M * 4 + M_TILES]
         nc.sync.dma_start(bias, b.rearrange("(m p) -> p m", p=P))
         nc.sync.dma_start(late[:, 0:N_TILE], wgo[:, 0:N_TILE])
         carry(1, N_TILE, S)
+        w_late = [late[:, S + 4 * P * a : S + 4 * P * (a + 1)].rearrange("p (j n) -> p j n", j=4) for a in range(PASSES)]
+        for a in range(PASSES):
+            load_w(w_late[a], a, 1)
+        w_raw = [[w_early[a][:], w_late[a]] for a in range(PASSES)]
+        nc.sync.dma_start(late[:, N_TILE:S], wgo[:, N_TILE:S])
 
         picked_first = hold.tile([P, S], U32, name="picked_first", align_bytes=64)
         nc.vector.tensor_copy(picked_first[:], words[0][:].bitcast(U32).indirect(list_in[:]))
-        weight_rest = hold.tile([P, S - N_TILE], F32, name="weight_rest", tag="words0", align_bytes=64)
-        nc.sync.dma_start(weight_rest[:], wgo[:, N_TILE:S])
 
         w_inter = [
             hold.tile([P, PASSES, P, 4], BF16, name=f"w_inter{m}", tag=f"turn{m}", align_bytes=64) for m in range(M_TILES)
         ]
         w_codes = hold.tile([P, M_TILES, PASSES, P], U32, name="w_codes", align_bytes=64)
         w_scales = hold.tile([P, M_TILES, PASSES, P], U8, name="w_scales", align_bytes=64)
-        for a in range(PASSES):
-            for m in range(M_TILES):
+        for m in range(M_TILES):
+            for a in range(PASSES):
                 nc.scalar.copy(
                     w_inter[m][:, a, :, :].rearrange("p (c i) j -> p c j i", i=4),
                     w_raw[a][m].rearrange("p j (c i) -> p c j i", i=4),
@@ -109,7 +112,7 @@ def tile_list_tabscat_silu_kernel(tc, tab, w, b, wgo, offs, offs2, out):
         def multiply(m, first, last, bank):
             acc = psum.tile([P, last - first], F32, name=f"acc{m}_{first}", tag=bank)
             part = 0 if first < N_TILE else 1
-            edges = [first] + ([CUT] if first < CUT < last else []) + [last]
+            edges = [first] + ([first + N_TILE // 2, CUT] if first < CUT < last else []) + [last]
             for lo, hi in zip(edges, edges[1:]):
                 rhs = [picked_first[:, lo:hi], picked_early[:, lo:hi] if lo < CUT else picked_late[:, lo - CUT : hi - CUT]]
                 for a in range(PASSES):
@@ -130,22 +133,23 @@ def tile_list_tabscat_silu_kernel(tc, tab, w, b, wgo, offs, offs2, out):
             nc.vector.tensor_tensor(
                 windows[m][:].indirect(list_out[:, COLS * first : COLS * last]),
                 results[m][:, cols],
-                late[:, 0:N_TILE] if first == 0 else weight_rest[:],
+                late[:, cols],
                 MULT,
             )
 
         picked_early = gather_last(0, CUT, "picked_early")
         quantise(0)
-        picked_late = gather_last(CUT, S, "w_last0")
+        picked_late = gather_last(CUT, S, "w_early1")
+        multiply(0, 0, 256, "bank0_0")
+        multiply(0, 256, 384, "bank1_3")
+        multiply(0, 384, N_TILE, "bank1_2")
+        for s in range(1, SLICES):
+            multiply(0, N_TILE * s, N_TILE * (s + 1), f"bank0_{s}")
+        scatter(0, 0, 1)
         quantise(1)
-        multiply(0, 0, N_TILE // 2, "bank0_0")
-        multiply(0, N_TILE // 2, N_TILE, "bank1_3")
-        multiply(1, 0, N_TILE, "bank1_0")
-        for m in range(M_TILES):
-            for s in range(1, SLICES):
-                multiply(m, N_TILE * s, N_TILE * (s + 1), f"bank{m}_{s}")
-        for m in range(M_TILES):
-            scatter(m, 0, 1)
-        for m in range(M_TILES):
-            scatter(m, 1, SLICES)
-            nc.sync.dma_start(out[P * m : P * (m + 1), :], windows[m][:])
+        for s in range(SLICES):
+            multiply(1, N_TILE * s, N_TILE * (s + 1), f"bank1_{s}")
+        scatter(0, 1, SLICES)
+        nc.sync.dma_start(out[0:P, :], windows[0][:])
+        scatter(1, 0, SLICES)
+        nc.sync.dma_start(out[P:M, :], windows[1][:])

@@ -45,10 +45,6 @@ def tile_list_tabscat_silu_kernel(tc, tab, w, b, wgo, offs, offs2, out):
             load_w(w_early[a][:], a, 0)
         nc.sync.dma_start(list_out[:], offs2)
 
-        warm = hold.tile([P, 2], F32, name="warm")
-        nc.gpsimd.memset(warm[:, 0:1], 0.0)
-        nc.scalar.activation(warm[:, 1:2], warm[:, 0:1], SILU)
-
         widths = [N_TILE, S - N_TILE]
         planes = [hold.tile([P, PASSES * width], U8, name=f"planes{i}", align_bytes=64) for i, width in enumerate(widths)]
         for plane in planes:

@@ -8,6 +8,7 @@ N_TILE = 512
 SLICES = S // N_TILE
 COLS = N_TILE // 16
 CUT = 896
+HEAD = 768
 
 F32 = mybir.dt.float32
 BF16 = mybir.dt.bfloat16
@@ -42,10 +43,12 @@ def tile_list_tabscat_silu_kernel(tc, tab, w, b, wgo, offs, offs2, out):
 
         w_early = [hold.tile([P, 4, P], F32, name=f"w_early{a}", tag=f"w_early{a}", align_bytes=64) for a in range(PASSES)]
         for a in range(PASSES):
-            load_w(w_early[a][:], a, 0)
-        nc.sync.dma_start(list_out[:], offs2)
+            load_w(w_early[a][:], a, 1)
+        w_late = [hold.tile([P, 4, P], F32, name=f"w_late{a}", tag=f"w_late{a}", align_bytes=64)[:] for a in range(PASSES)]
+        for a in range(PASSES):
+            load_w(w_late[a], a, 0)
 
-        widths = [N_TILE, S - N_TILE]
+        widths = [HEAD, S - HEAD]
         planes = [hold.tile([P, PASSES * width], U8, name=f"planes{i}", align_bytes=64) for i, width in enumerate(widths)]
         for plane in planes:
             nc.gpsimd.memset(plane[:].bitcast(I32), 0)
@@ -64,17 +67,15 @@ def tile_list_tabscat_silu_kernel(tc, tab, w, b, wgo, offs, offs2, out):
                     picked_rows[96 + 8 * quad : 96 + 8 * quad + 8, first // 4 : last // 4],
                 )
 
-        carry(0, 0, N_TILE)
+        carry(0, 0, HEAD)
+        nc.sync.dma_start(list_out[:], offs2)
         late = hold.tile([P, S + M * 4 + 8], F32, name="late", tag="scales", align_bytes=64)
         bias = late[:, S + M * 4 : S + M * 4 + M_TILES]
         nc.sync.dma_start(bias, b.rearrange("(m p) -> p m", p=P))
-        nc.sync.dma_start(late[:, 0:N_TILE], wgo[:, 0:N_TILE])
-        carry(1, N_TILE, S)
-        w_late = [late[:, S + 4 * P * a : S + 4 * P * (a + 1)].rearrange("p (j n) -> p j n", j=4) for a in range(PASSES)]
-        for a in range(PASSES):
-            load_w(w_late[a], a, 1)
-        w_raw = [[w_early[a][:], w_late[a]] for a in range(PASSES)]
-        nc.sync.dma_start(late[:, N_TILE:S], wgo[:, N_TILE:S])
+        nc.sync.dma_start(late[:, 0:HEAD], wgo[:, 0:HEAD])
+        carry(1, HEAD, S)
+        w_raw = [[w_late[a], w_early[a][:]] for a in range(PASSES)]
+        nc.sync.dma_start(late[:, HEAD:S], wgo[:, HEAD:S])
 
         picked_first = hold.tile([P, S], U32, name="picked_first", align_bytes=64)
         nc.vector.tensor_copy(picked_first[:], words[0][:].bitcast(U32).indirect(list_in[:]))
@@ -84,7 +85,9 @@ def tile_list_tabscat_silu_kernel(tc, tab, w, b, wgo, offs, offs2, out):
         ]
         w_codes = hold.tile([P, M_TILES, PASSES, P], U32, name="w_codes", align_bytes=64)
         w_scales = hold.tile([P, M_TILES, PASSES, P], U8, name="w_scales", align_bytes=64)
-        for m in range(M_TILES):
+        warm = hold.tile([P, 8], F32, name="warm")
+        nc.scalar.activation(warm[:, 0:1], windows[0][:, 0:1], SILU)
+        for m in (1, 0):
             for a in range(PASSES):
                 nc.scalar.copy(
                     w_inter[m][:, a, :, :].rearrange("p (c i) j -> p c j i", i=4),
@@ -103,16 +106,17 @@ def tile_list_tabscat_silu_kernel(tc, tab, w, b, wgo, offs, offs2, out):
             nc.vector.tensor_copy(part[:], words[1][:].bitcast(U32).indirect(list_in[:, first // 16 : last // 16]))
             return part
 
+        opening = hold.tile([P, HEAD], F32, name="opening", tag="w_late1", align_bytes=64)
         results = [hold.tile([P, S], F32, name=f"result{m}") for m in range(M_TILES)]
 
         def multiply(m, first, last, bank):
             acc = psum.tile([P, last - first], F32, name=f"acc{m}_{first}", tag=bank)
-            part = 0 if first < N_TILE else 1
-            edges = [first] + ([first + N_TILE // 2, CUT] if first < CUT < last else []) + [last]
+            edges = [first] + [edge for edge in (HEAD, CUT) if first < edge < last] + [last]
             for lo, hi in zip(edges, edges[1:]):
+                part = 0 if lo < HEAD else 1
                 rhs = [picked_first[:, lo:hi], picked_early[:, lo:hi] if lo < CUT else picked_late[:, lo - CUT : hi - CUT]]
                 for a in range(PASSES):
-                    at = widths[part] * a - N_TILE * part
+                    at = widths[part] * a - HEAD * part
                     nc.tensor.matmul_mx(
                         out=acc[:, lo - first : hi - first],
                         lhsT=w_codes[:, m, a, :].bitcast(FP8X4),
@@ -122,30 +126,33 @@ def tile_list_tabscat_silu_kernel(tc, tab, w, b, wgo, offs, offs2, out):
                         start=(a == 0),
                         stop=(a == PASSES - 1),
                     )
-            nc.scalar.activation(results[m][:, first:last], acc[:], SILU, bias=bias[:, m : m + 1])
+            target = opening if (m == 1 and last <= HEAD) else results[m]
+            nc.scalar.activation(target[:, first:last], acc[:], SILU, bias=bias[:, m : m + 1])
 
         def scatter(m, first, last):
-            cols = slice(N_TILE * first, N_TILE * last)
+            cols = slice(first, last)
             nc.vector.tensor_tensor(
-                windows[m][:].indirect(list_out[:, COLS * first : COLS * last]),
-                results[m][:, cols],
+                windows[m][:].indirect(list_out[:, first // 16 : last // 16]),
+                opening[:] if (m == 1 and last == HEAD) else results[m][:, cols],
                 late[:, cols],
                 MULT,
             )
 
         picked_early = gather_last(0, CUT, "picked_early")
-        quantise(0)
-        picked_late = gather_last(CUT, S, "w_early1")
-        multiply(0, 0, 256, "bank0_0")
-        multiply(0, 256, 384, "bank1_3")
-        multiply(0, 384, N_TILE, "bank1_2")
-        for s in range(1, SLICES):
-            multiply(0, N_TILE * s, N_TILE * (s + 1), f"bank0_{s}")
-        scatter(0, 0, 1)
         quantise(1)
+        picked_late = gather_last(CUT, S, "w_early1")
+        multiply(1, 0, 256, "bank1_0")
+        multiply(1, 256, 512, "bank1_3")
+        multiply(1, 512, 640, "bank1_2")
+        multiply(1, 640, HEAD, "bank1_1")
+        quantise(0)
         for s in range(SLICES):
+            multiply(0, N_TILE * s, N_TILE * (s + 1), f"bank0_{s}")
+        scatter(1, 0, HEAD)
+        multiply(1, HEAD, 2 * N_TILE, "bank1_0")
+        for s in range(2, SLICES):
             multiply(1, N_TILE * s, N_TILE * (s + 1), f"bank1_{s}")
-        scatter(0, 1, SLICES)
+        scatter(0, 0, S)
         nc.sync.dma_start(out[0:P, :], windows[0][:])
-        scatter(1, 0, SLICES)
+        scatter(1, HEAD, S)
         nc.sync.dma_start(out[P:M, :], windows[1][:])

@@ -35,7 +35,7 @@ def tile_list_tabscat_silu_kernel(tc, tab, w, b, wgo, offs, offs2, out):
         nc.sync.dma_start(scale_words[96:P, :], tab[:, 512 * T : 528 * T].rearrange("a (q t) -> q a t", q=16).bitcast(I32))
         nc.sync.dma_start(list_in[:], offs)
 
-        words = [hold.tile([P, T], I32, name=f"words{a}", align_bytes=64) for a in range(PASSES)]
+        words = [hold.tile([P, T], I32, name=f"words{a}", tag=f"words{a}", align_bytes=64) for a in range(PASSES)]
         for a in range(PASSES):
             nc.sync.dma_start(words[a][:], tab[a, 0 : 512 * T].rearrange("(p x) -> p x", p=P).bitcast(I32))
         def load_w(tile, a, m):
@@ -44,9 +44,9 @@ def tile_list_tabscat_silu_kernel(tc, tab, w, b, wgo, offs, offs2, out):
         w_early = [hold.tile([P, 4, P], F32, name=f"w_early{a}", tag=f"w_early{a}", align_bytes=64) for a in range(PASSES)]
         for a in range(PASSES):
             load_w(w_early[a][:], a, 1)
-        w_late = [hold.tile([P, 4, P], F32, name=f"w_late{a}", tag=f"w_late{a}", align_bytes=64)[:] for a in range(PASSES)]
-        for a in range(PASSES):
-            load_w(w_late[a], a, 0)
+        nc.sync.dma_start(list_out[:], offs2)
+        bias = hold.tile([P, M_TILES], F32, name="bias")
+        nc.sync.dma_start(bias[:], b.rearrange("(m p) -> p m", p=P))
 
         widths = [HEAD, S - HEAD]
         planes = [hold.tile([P, PASSES * width], U8, name=f"planes{i}", align_bytes=64) for i, width in enumerate(widths)]
@@ -68,17 +68,18 @@ def tile_list_tabscat_silu_kernel(tc, tab, w, b, wgo, offs, offs2, out):
                 )
 
         carry(0, 0, HEAD)
-        nc.sync.dma_start(list_out[:], offs2)
-        late = hold.tile([P, S + M * 4 + 8], F32, name="late", tag="scales", align_bytes=64)
-        bias = late[:, S + M * 4 : S + M * 4 + M_TILES]
-        nc.sync.dma_start(bias, b.rearrange("(m p) -> p m", p=P))
+        w_pair = hold.tile([P, PASSES * 4 * P], F32, name="w_pair", tag="scales", align_bytes=64)
+        w_late = [w_pair[:, 4 * P * a : 4 * P * (a + 1)].rearrange("p (j n) -> p j n", j=4) for a in range(PASSES)]
+        for a in range(PASSES):
+            load_w(w_late[a], a, 0)
+        picked_first = hold.tile([P, S], U32, name="picked_first", align_bytes=64)
+        nc.vector.tensor_copy(picked_first[:], words[0][:].bitcast(U32).indirect(list_in[:]))
+        late = hold.tile([P, S], F32, name="late", tag="words0", align_bytes=64)
         nc.sync.dma_start(late[:, 0:HEAD], wgo[:, 0:HEAD])
         carry(1, HEAD, S)
         w_raw = [[w_late[a], w_early[a][:]] for a in range(PASSES)]
         nc.sync.dma_start(late[:, HEAD:S], wgo[:, HEAD:S])
 
-        picked_first = hold.tile([P, S], U32, name="picked_first", align_bytes=64)
-        nc.vector.tensor_copy(picked_first[:], words[0][:].bitcast(U32).indirect(list_in[:]))
 
         w_inter = [
             hold.tile([P, PASSES, P, 4], BF16, name=f"w_inter{m}", tag=f"turn{m}", align_bytes=64) for m in range(M_TILES)
@@ -106,7 +107,7 @@ def tile_list_tabscat_silu_kernel(tc, tab, w, b, wgo, offs, offs2, out):
             nc.vector.tensor_copy(part[:], words[1][:].bitcast(U32).indirect(list_in[:, first // 16 : last // 16]))
             return part
 
-        opening = hold.tile([P, HEAD], F32, name="opening", tag="w_late1", align_bytes=64)
+        opening = hold.tile([P, HEAD], F32, name="opening", tag="scales", align_bytes=64)
         results = [hold.tile([P, S], F32, name=f"result{m}") for m in range(M_TILES)]
 
         def multiply(m, first, last, bank):

@@ -26,22 +26,22 @@ FLOPS = 2 * K * M * S
 def tile_list_tabscat_silu_kernel(tc, tab, w, b, wgo, offs, offs2, out):
     nc = tc.nc
     with tc.tile_pool(name="hold", bufs=1) as hold, tc.psum_pool(name="psum", bufs=1) as psum:
-        list_in = hold.tile([P, S // 16], U16, name="list_in")
-        list_out = hold.tile([P, S // 16], U16, name="list_out")
+        list_in = hold.tile([P, S // 16], U16, name="list_in", align_bytes=256)
+        list_out = hold.tile([P, S // 16], U16, name="list_out", align_bytes=256)
 
-        scales = hold.tile([P, T], U8, name="scales", align_bytes=64)
+        scales = hold.tile([P, T], U8, name="scales", align_bytes=256)
         scale_words = scales[:].bitcast(I32)
         nc.gpsimd.memset(scale_words[0:96, :], 0)
         nc.sync.dma_start(scale_words[96:P, :], tab[:, 512 * T : 528 * T].rearrange("a (q t) -> q a t", q=16).bitcast(I32))
         nc.sync.dma_start(list_in[:], offs)
 
-        words = [hold.tile([P, T], I32, name=f"words{a}", tag=f"words{a}", align_bytes=64) for a in range(PASSES)]
+        words = [hold.tile([P, T], I32, name=f"words{a}", tag=f"words{a}", align_bytes=256) for a in range(PASSES)]
         for a in range(PASSES):
             nc.sync.dma_start(words[a][:], tab[a, 0 : 512 * T].rearrange("(p x) -> p x", p=P).bitcast(I32))
         def load_w(tile, a, m):
             nc.sync.dma_start(tile, w[512 * a : 512 * (a + 1), P * m : P * (m + 1)].rearrange("(p j) n -> p j n", j=4))
 
-        w_early = [hold.tile([P, 4, P], F32, name=f"w_early{a}", tag=f"w_early{a}", align_bytes=64) for a in range(PASSES)]
+        w_early = [hold.tile([P, 4, P], F32, name=f"w_early{a}", tag=f"w_early{a}", align_bytes=256) for a in range(PASSES)]
         for a in range(PASSES):
             load_w(w_early[a][:], a, 1)
         nc.sync.dma_start(list_out[:], offs2)
@@ -49,14 +49,14 @@ def tile_list_tabscat_silu_kernel(tc, tab, w, b, wgo, offs, offs2, out):
         nc.sync.dma_start(bias[:], b.rearrange("(m p) -> p m", p=P))
 
         widths = [HEAD, S - HEAD]
-        planes = [hold.tile([P, PASSES * width], U8, name=f"planes{i}", align_bytes=64) for i, width in enumerate(widths)]
+        planes = [hold.tile([P, PASSES * width], U8, name=f"planes{i}", align_bytes=256) for i, width in enumerate(widths)]
         for plane in planes:
             nc.gpsimd.memset(plane[:].bitcast(I32), 0)
-        windows = [hold.tile([P, T], F32, name=f"window{m}") for m in range(M_TILES)]
+        windows = [hold.tile([P, T], F32, name=f"window{m}", align_bytes=256) for m in range(M_TILES)]
         for m in range(M_TILES):
             nc.gpsimd.memset(windows[m][:], 0.0)
 
-        picked_scales = hold.tile([P, S], U8, name="picked_scales", align_bytes=64)
+        picked_scales = hold.tile([P, S], U8, name="picked_scales", align_bytes=256)
         nc.vector.tensor_copy(picked_scales[:], scales[:].indirect(list_in[:]))
         picked_rows = picked_scales[:].bitcast(I32)
 
@@ -68,13 +68,13 @@ def tile_list_tabscat_silu_kernel(tc, tab, w, b, wgo, offs, offs2, out):
                 )
 
         carry(0, 0, HEAD)
-        w_pair = hold.tile([P, PASSES * 4 * P], F32, name="w_pair", tag="scales", align_bytes=64)
+        w_pair = hold.tile([P, PASSES * 4 * P], F32, name="w_pair", tag="scales", align_bytes=256)
         w_late = [w_pair[:, 4 * P * a : 4 * P * (a + 1)].rearrange("p (j n) -> p j n", j=4) for a in range(PASSES)]
         for a in range(PASSES):
             load_w(w_late[a], a, 0)
-        picked_first = hold.tile([P, S], U32, name="picked_first", align_bytes=64)
+        picked_first = hold.tile([P, S], U32, name="picked_first", align_bytes=256)
         nc.vector.tensor_copy(picked_first[:], words[0][:].bitcast(U32).indirect(list_in[:]))
-        late = hold.tile([P, S], F32, name="late", tag="words0", align_bytes=64)
+        late = hold.tile([P, S], F32, name="late", tag="words0", align_bytes=256)
         nc.sync.dma_start(late[:, 0:HEAD], wgo[:, 0:HEAD])
         carry(1, HEAD, S)
         w_raw = [[w_late[a], w_early[a][:]] for a in range(PASSES)]
@@ -82,10 +82,10 @@ def tile_list_tabscat_silu_kernel(tc, tab, w, b, wgo, offs, offs2, out):
 
 
         w_inter = [
-            hold.tile([P, PASSES, P, 4], BF16, name=f"w_inter{m}", tag=f"turn{m}", align_bytes=64) for m in range(M_TILES)
+            hold.tile([P, PASSES, P, 4], BF16, name=f"w_inter{m}", tag=f"turn{m}", align_bytes=256) for m in range(M_TILES)
         ]
-        w_codes = hold.tile([P, M_TILES, PASSES, P], U32, name="w_codes", align_bytes=64)
-        w_scales = hold.tile([P, M_TILES, PASSES, P], U8, name="w_scales", align_bytes=64)
+        w_codes = hold.tile([P, M_TILES, PASSES, P], U32, name="w_codes", align_bytes=256)
+        w_scales = hold.tile([P, M_TILES, PASSES, P], U8, name="w_scales", align_bytes=256)
         warm = hold.tile([P, 8], F32, name="warm")
         nc.scalar.activation(warm[:, 0:1], windows[0][:, 0:1], SILU)
         for m in (1, 0):
@@ -103,12 +103,12 @@ def tile_list_tabscat_silu_kernel(tc, tab, w, b, wgo, offs, offs2, out):
             )
 
         def gather_last(first, last, tag):
-            part = hold.tile([P, last - first], U32, name=f"picked_last{first}", tag=tag, align_bytes=64)
+            part = hold.tile([P, last - first], U32, name=f"picked_last{first}", tag=tag, align_bytes=256)
             nc.vector.tensor_copy(part[:], words[1][:].bitcast(U32).indirect(list_in[:, first // 16 : last // 16]))
             return part
 
-        opening = hold.tile([P, HEAD], F32, name="opening", tag="scales", align_bytes=64)
-        results = [hold.tile([P, S], F32, name=f"result{m}") for m in range(M_TILES)]
+        opening = hold.tile([P, HEAD], F32, name="opening", tag="scales", align_bytes=256)
+        results = [hold.tile([P, S], F32, name=f"result{m}", align_bytes=256) for m in range(M_TILES)]
 
         def multiply(m, first, last, bank):
             acc = psum.tile([P, last - first], F32, name=f"acc{m}_{first}", tag=bank)

@@ -87,7 +87,8 @@ def tile_list_tabscat_silu_kernel(tc, tab, w, b, wgo, offs, offs2, out):
         w_codes = hold.tile([P, M_TILES, PASSES, P], U32, name="w_codes", align_bytes=256)
         w_scales = hold.tile([P, M_TILES, PASSES, P], U8, name="w_scales", align_bytes=256)
         warm = hold.tile([P, 8], F32, name="warm")
-        nc.scalar.activation(warm[:, 0:1], windows[0][:, 0:1], SILU)
+        nc.gpsimd.memset(warm[:, 0:1], 0.0)
+        nc.scalar.activation(warm[:, 1:2], warm[:, 0:1], SILU)
         for m in (1, 0):
             for a in range(PASSES):
                 nc.scalar.copy(

@@ -35,7 +35,7 @@ def tile_list_tabscat_silu_kernel(tc, tab, w, b, wgo, offs, offs2, out):
         nc.sync.dma_start(scale_words[96:P, :], tab[:, 512 * T : 528 * T].rearrange("a (q t) -> q a t", q=16).bitcast(I32))
         nc.sync.dma_start(list_in[:], offs)
 
-        words = [hold.tile([P, T], I32, name=f"words{a}", tag=f"words{a}", align_bytes=256) for a in range(PASSES)]
+        words = [hold.tile([P, T], I32, name=f"words{a}", tag=f"words{a}", align_bytes=4096) for a in range(PASSES)]
         for a in range(PASSES):
             nc.sync.dma_start(words[a][:], tab[a, 0 : 512 * T].rearrange("(p x) -> p x", p=P).bitcast(I32))
         def load_w(tile, a, m):
@@ -52,7 +52,7 @@ def tile_list_tabscat_silu_kernel(tc, tab, w, b, wgo, offs, offs2, out):
         planes = [hold.tile([P, PASSES * width], U8, name=f"planes{i}", align_bytes=256) for i, width in enumerate(widths)]
         for plane in planes:
             nc.gpsimd.memset(plane[:].bitcast(I32), 0)
-        windows = [hold.tile([P, T], F32, name=f"window{m}", align_bytes=256) for m in range(M_TILES)]
+        windows = [hold.tile([P, T], F32, name=f"window{m}", align_bytes=4096) for m in range(M_TILES)]
         for m in range(M_TILES):
             nc.gpsimd.memset(windows[m][:], 0.0)
 
@@ -74,7 +74,7 @@ def tile_list_tabscat_silu_kernel(tc, tab, w, b, wgo, offs, offs2, out):
             load_w(w_late[a], a, 0)
         picked_first = hold.tile([P, S], U32, name="picked_first", align_bytes=256)
         nc.vector.tensor_copy(picked_first[:], words[0][:].bitcast(U32).indirect(list_in[:]))
-        late = hold.tile([P, S], F32, name="late", tag="words0", align_bytes=256)
+        late = hold.tile([P, S], F32, name="late", tag="words0", align_bytes=4096)
         nc.sync.dma_start(late[:, 0:HEAD], wgo[:, 0:HEAD])
         carry(1, HEAD, S)
         w_raw = [[w_late[a], w_early[a][:]] for a in range(PASSES)]

@@ -4,11 +4,10 @@ K, M, T, S = 1024, 256, 4096, 2048
 P = 128
 PASSES = K // 512
 M_TILES = M // P
-N_TILE = 512
-SLICES = S // N_TILE
-COLS = N_TILE // 16
-CUT = 896
-HEAD = 768
+BANK = 512
+HEAD = 896
+KIB = 1024
+SHARE = 1920
 
 F32 = mybir.dt.float32
 BF16 = mybir.dt.bfloat16
@@ -23,21 +22,42 @@ SILU = mybir.ActivationFunctionType.Silu
 FLOPS = 2 * K * M * S
 
 
+def runs(first, last):
+    pieces = []
+    while first < last:
+        stop = min(last, HEAD) if first < HEAD else last
+        width = max(n for n in (128, 256, 512) if first + n <= stop)
+        pieces.append((first, first + width))
+        first += width
+    return pieces
+
+
 def tile_list_tabscat_silu_kernel(tc, tab, w, b, wgo, offs, offs2, out):
     nc = tc.nc
-    with tc.tile_pool(name="hold", bufs=1) as hold, tc.psum_pool(name="psum", bufs=1) as psum:
+    with (
+        tc.tile_pool(name="hold", bufs=1) as hold,
+        tc.tile_pool(name="shared", bufs=1) as shared,
+        tc.psum_pool(name="psum", bufs=1) as psum,
+    ):
         list_in = hold.tile([P, S // 16], U16, name="list_in", align_bytes=256)
         list_out = hold.tile([P, S // 16], U16, name="list_out", align_bytes=256)
 
-        scales = hold.tile([P, T], U8, name="scales", align_bytes=256)
+        scales = shared.tile([P, T], U8, name="scales", offset=0, align_bytes=256)
         scale_words = scales[:].bitcast(I32)
         nc.gpsimd.memset(scale_words[0:96, :], 0)
         nc.sync.dma_start(scale_words[96:P, :], tab[:, 512 * T : 528 * T].rearrange("a (q t) -> q a t", q=16).bitcast(I32))
         nc.sync.dma_start(list_in[:], offs)
+        window_first = hold.tile([P, T], F32, name="window_first", align_bytes=4096)
+        nc.vector.memset(window_first[:, 0 : SHARE - 1], 0.0)
+        nc.vector.memset(window_first[:, SHARE - 1 : SHARE], 0.0)
+        nc.gpsimd.memset(window_first[:, SHARE:T], 0.0)
 
-        words = [hold.tile([P, T], I32, name=f"words{a}", tag=f"words{a}", align_bytes=4096) for a in range(PASSES)]
+        words = [
+            shared.tile([P, T], I32, name=f"words{a}", offset=(8 + 16 * a) * KIB, align_bytes=256) for a in range(PASSES)
+        ]
         for a in range(PASSES):
             nc.sync.dma_start(words[a][:], tab[a, 0 : 512 * T].rearrange("(p x) -> p x", p=P).bitcast(I32))
+
         def load_w(tile, a, m):
             nc.sync.dma_start(tile, w[512 * a : 512 * (a + 1), P * m : P * (m + 1)].rearrange("(p j) n -> p j n", j=4))
 
@@ -48,17 +68,15 @@ def tile_list_tabscat_silu_kernel(tc, tab, w, b, wgo, offs, offs2, out):
         bias = hold.tile([P, M_TILES], F32, name="bias")
         nc.sync.dma_start(bias[:], b.rearrange("(m p) -> p m", p=P))
 
-        widths = [HEAD, S - HEAD]
-        planes = [hold.tile([P, PASSES * width], U8, name=f"planes{i}", align_bytes=256) for i, width in enumerate(widths)]
-        for plane in planes:
-            nc.gpsimd.memset(plane[:].bitcast(I32), 0)
-        windows = [hold.tile([P, T], F32, name=f"window{m}", align_bytes=4096) for m in range(M_TILES)]
-        for m in range(M_TILES):
-            nc.gpsimd.memset(windows[m][:], 0.0)
-
         picked_scales = hold.tile([P, S], U8, name="picked_scales", align_bytes=256)
         nc.vector.tensor_copy(picked_scales[:], scales[:].indirect(list_in[:]))
         picked_rows = picked_scales[:].bitcast(I32)
+
+        widths = [HEAD, S - HEAD]
+        planes = [
+            shared.tile([P, PASSES * widths[0]], U8, name="planes_head", offset=0, align_bytes=256),
+            shared.tile([P, PASSES * widths[1]], U8, name="planes_rest", offset=16 * KIB, align_bytes=256),
+        ]
 
         def carry(part, first, last):
             for quad in range(4):
@@ -68,21 +86,20 @@ def tile_list_tabscat_silu_kernel(tc, tab, w, b, wgo, offs, offs2, out):
                 )
 
         carry(0, 0, HEAD)
-        w_pair = hold.tile([P, PASSES * 4 * P], F32, name="w_pair", tag="scales", align_bytes=256)
+        w_pair = shared.tile([P, PASSES * 4 * P], F32, name="w_pair", offset=2 * KIB, align_bytes=256)
         w_late = [w_pair[:, 4 * P * a : 4 * P * (a + 1)].rearrange("p (j n) -> p j n", j=4) for a in range(PASSES)]
         for a in range(PASSES):
             load_w(w_late[a], a, 0)
         picked_first = hold.tile([P, S], U32, name="picked_first", align_bytes=256)
         nc.vector.tensor_copy(picked_first[:], words[0][:].bitcast(U32).indirect(list_in[:]))
-        late = hold.tile([P, S], F32, name="late", tag="words0", align_bytes=4096)
-        nc.sync.dma_start(late[:, 0:HEAD], wgo[:, 0:HEAD])
+        gate = shared.tile([P, S], F32, name="gate", offset=8 * KIB, align_bytes=256)
+        nc.sync.dma_start(gate[:, 0:HEAD], wgo[:, 0:HEAD])
         carry(1, HEAD, S)
+        nc.sync.dma_start(gate[:, HEAD:S], wgo[:, HEAD:S])
         w_raw = [[w_late[a], w_early[a][:]] for a in range(PASSES)]
-        nc.sync.dma_start(late[:, HEAD:S], wgo[:, HEAD:S])
-
 
         w_inter = [
-            hold.tile([P, PASSES, P, 4], BF16, name=f"w_inter{m}", tag=f"turn{m}", align_bytes=256) for m in range(M_TILES)
+            hold.tile([P, PASSES, P, 4], BF16, name=f"w_inter{m}", tag=f"turn{m}", align_bytes=4096) for m in range(M_TILES)
         ]
         w_codes = hold.tile([P, M_TILES, PASSES, P], U32, name="w_codes", align_bytes=256)
         w_scales = hold.tile([P, M_TILES, PASSES, P], U8, name="w_scales", align_bytes=256)
@@ -108,15 +125,14 @@ def tile_list_tabscat_silu_kernel(tc, tab, w, b, wgo, offs, offs2, out):
             nc.vector.tensor_copy(part[:], words[1][:].bitcast(U32).indirect(list_in[:, first // 16 : last // 16]))
             return part
 
-        opening = hold.tile([P, HEAD], F32, name="opening", tag="scales", align_bytes=256)
+        opening = shared.tile([P, HEAD], F32, name="opening", offset=2 * KIB, align_bytes=256)
         results = [hold.tile([P, S], F32, name=f"result{m}", align_bytes=256) for m in range(M_TILES)]
 
         def multiply(m, first, last, bank):
             acc = psum.tile([P, last - first], F32, name=f"acc{m}_{first}", tag=bank)
-            edges = [first] + [edge for edge in (HEAD, CUT) if first < edge < last] + [last]
-            for lo, hi in zip(edges, edges[1:]):
+            for lo, hi in runs(first, last):
                 part = 0 if lo < HEAD else 1
-                rhs = [picked_first[:, lo:hi], picked_early[:, lo:hi] if lo < CUT else picked_late[:, lo - CUT : hi - CUT]]
+                rhs = [picked_first[:, lo:hi], picked_last[part][:, lo - HEAD * part : hi - HEAD * part]]
                 for a in range(PASSES):
                     at = widths[part] * a - HEAD * part
                     nc.tensor.matmul_mx(
@@ -131,30 +147,26 @@ def tile_list_tabscat_silu_kernel(tc, tab, w, b, wgo, offs, offs2, out):
             target = opening if (m == 1 and last <= HEAD) else results[m]
             nc.scalar.activation(target[:, first:last], acc[:], SILU, bias=bias[:, m : m + 1])
 
-        def scatter(m, first, last):
-            cols = slice(first, last)
+        def scatter(window, values, first, last):
             nc.vector.tensor_tensor(
-                windows[m][:].indirect(list_out[:, first // 16 : last // 16]),
-                opening[:] if (m == 1 and last == HEAD) else results[m][:, cols],
-                late[:, cols],
-                MULT,
+                window[:].indirect(list_out[:, first // 16 : last // 16]), values, gate[:, first:last], MULT
             )
 
-        picked_early = gather_last(0, CUT, "picked_early")
+        picked_last = [gather_last(0, HEAD, "picked_early")]
         quantise(1)
-        picked_late = gather_last(CUT, S, "w_early1")
-        multiply(1, 0, 256, "bank1_0")
-        multiply(1, 256, 512, "bank1_3")
-        multiply(1, 512, 640, "bank1_2")
-        multiply(1, 640, HEAD, "bank1_1")
+        picked_last.append(gather_last(HEAD, S, "w_early1"))
+        for i, (first, last) in enumerate(((0, 256), (256, 512), (512, 768), (768, HEAD))):
+            multiply(1, first, last, f"bank1_{i}")
         quantise(0)
-        for s in range(SLICES):
-            multiply(0, N_TILE * s, N_TILE * (s + 1), f"bank0_{s}")
-        scatter(1, 0, HEAD)
-        multiply(1, HEAD, 2 * N_TILE, "bank1_0")
-        for s in range(2, SLICES):
-            multiply(1, N_TILE * s, N_TILE * (s + 1), f"bank1_{s}")
-        scatter(0, 0, S)
-        nc.sync.dma_start(out[0:P, :], windows[0][:])
-        scatter(1, HEAD, S)
-        nc.sync.dma_start(out[P:M, :], windows[1][:])
+        window_second = hold.tile([P, T], F32, name="window_second", tag="turn0", align_bytes=4096)
+        nc.gpsimd.memset(window_second[:], 0.0)
+        for s in range(S // BANK):
+            multiply(0, BANK * s, BANK * (s + 1), f"bank0_{s}")
+        scatter(window_first, opening[:], 0, HEAD)
+        multiply(1, HEAD, 2 * BANK, "bank1_0")
+        for s in range(2, S // BANK):
+            multiply(1, BANK * s, BANK * (s + 1), f"bank1_{s}")
+        scatter(window_second, results[0][:], 0, S)
+        nc.sync.dma_start(out[0:P, :], window_second[:])
+        scatter(window_first, results[1][:, HEAD:S], HEAD, S)
+        nc.sync.dma_start(out[P:M, :], window_first[:])

@@ -95,7 +95,8 @@ def tile_list_tabscat_silu_kernel(tc, tab, w, b, wgo, offs, offs2, out):
         gate = shared.tile([P, S], F32, name="gate", offset=8 * KIB, align_bytes=256)
         nc.sync.dma_start(gate[:, 0:HEAD], wgo[:, 0:HEAD])
         carry(1, HEAD, S)
-        nc.sync.dma_start(gate[:, HEAD:S], wgo[:, HEAD:S])
+        for first in range(HEAD, S, (S - HEAD) // 3):
+            nc.sync.dma_start(gate[:, first : first + (S - HEAD) // 3], wgo[:, first : first + (S - HEAD) // 3])
         w_raw = [[w_late[a], w_early[a][:]] for a in range(PASSES)]
 
         w_inter = [

@@ -7,7 +7,7 @@ M_TILES = M // P
 BANK = 512
 HEAD = 896
 KIB = 1024
-SHARE = 1920
+SHARE = 1280
 
 F32 = mybir.dt.float32
 BF16 = mybir.dt.bfloat16

import concourse.mybir as mybir

K, M, T, S = 1024, 256, 4096, 2048
P = 128
PASSES = K // 512
M_TILES = M // P
BANK = 512
HEAD = 896
KIB = 1024
SHARE = 1280

F32 = mybir.dt.float32
BF16 = mybir.dt.bfloat16
I32 = mybir.dt.int32
U32 = mybir.dt.uint32
U16 = mybir.dt.uint16
U8 = mybir.dt.uint8
FP8X4 = mybir.dt.float8_e4m3fn_x4
MULT = mybir.AluOpType.mult
SILU = mybir.ActivationFunctionType.Silu

FLOPS = 2 * K * M * S


def runs(first, last):
    pieces = []
    while first < last:
        stop = min(last, HEAD) if first < HEAD else last
        width = max(n for n in (128, 256, 512) if first + n <= stop)
        pieces.append((first, first + width))
        first += width
    return pieces


def tile_list_tabscat_silu_kernel(tc, tab, w, b, wgo, offs, offs2, out):
    nc = tc.nc
    with (
        tc.tile_pool(name="hold", bufs=1) as hold,
        tc.tile_pool(name="shared", bufs=1) as shared,
        tc.psum_pool(name="psum", bufs=1) as psum,
    ):
        list_in = hold.tile([P, S // 16], U16, name="list_in", align_bytes=256)
        list_out = hold.tile([P, S // 16], U16, name="list_out", align_bytes=256)

        scales = shared.tile([P, T], U8, name="scales", offset=0, align_bytes=256)
        scale_words = scales[:].bitcast(I32)
        nc.gpsimd.memset(scale_words[0:96, :], 0)
        nc.sync.dma_start(scale_words[96:P, :], tab[:, 512 * T : 528 * T].rearrange("a (q t) -> q a t", q=16).bitcast(I32))
        nc.sync.dma_start(list_in[:], offs)
        window_first = hold.tile([P, T], F32, name="window_first", align_bytes=4096)
        nc.vector.memset(window_first[:, 0 : SHARE - 1], 0.0)
        nc.vector.memset(window_first[:, SHARE - 1 : SHARE], 0.0)
        nc.gpsimd.memset(window_first[:, SHARE:T], 0.0)

        words = [
            shared.tile([P, T], I32, name=f"words{a}", offset=(8 + 16 * a) * KIB, align_bytes=256) for a in range(PASSES)
        ]
        for a in range(PASSES):
            nc.sync.dma_start(words[a][:], tab[a, 0 : 512 * T].rearrange("(p x) -> p x", p=P).bitcast(I32))

        def load_w(tile, a, m):
            nc.sync.dma_start(tile, w[512 * a : 512 * (a + 1), P * m : P * (m + 1)].rearrange("(p j) n -> p j n", j=4))

        w_early = [hold.tile([P, 4, P], F32, name=f"w_early{a}", tag=f"w_early{a}", align_bytes=256) for a in range(PASSES)]
        for a in range(PASSES):
            load_w(w_early[a][:], a, 1)
        nc.sync.dma_start(list_out[:], offs2)
        bias = hold.tile([P, M_TILES], F32, name="bias")
        nc.sync.dma_start(bias[:], b.rearrange("(m p) -> p m", p=P))

        picked_scales = hold.tile([P, S], U8, name="picked_scales", align_bytes=256)
        nc.vector.tensor_copy(picked_scales[:], scales[:].indirect(list_in[:]))
        picked_rows = picked_scales[:].bitcast(I32)

        widths = [HEAD, S - HEAD]
        planes = [
            shared.tile([P, PASSES * widths[0]], U8, name="planes_head", offset=0, align_bytes=256),
            shared.tile([P, PASSES * widths[1]], U8, name="planes_rest", offset=16 * KIB, align_bytes=256),
        ]

        def carry(part, first, last):
            for quad in range(4):
                nc.sync.dma_start(
                    planes[part][:].bitcast(I32)[32 * quad : 32 * quad + 4, :],
                    picked_rows[96 + 8 * quad : 96 + 8 * quad + 8, first // 4 : last // 4],
                )

        carry(0, 0, HEAD)
        w_pair = shared.tile([P, PASSES * 4 * P], F32, name="w_pair", offset=2 * KIB, align_bytes=256)
        w_late = [w_pair[:, 4 * P * a : 4 * P * (a + 1)].rearrange("p (j n) -> p j n", j=4) for a in range(PASSES)]
        for a in range(PASSES):
            load_w(w_late[a], a, 0)
        picked_first = hold.tile([P, S], U32, name="picked_first", align_bytes=256)
        nc.vector.tensor_copy(picked_first[:], words[0][:].bitcast(U32).indirect(list_in[:]))
        gate = shared.tile([P, S], F32, name="gate", offset=8 * KIB, align_bytes=256)
        nc.sync.dma_start(gate[:, 0:HEAD], wgo[:, 0:HEAD])
        carry(1, HEAD, S)
        for first in range(HEAD, S, (S - HEAD) // 3):
            nc.sync.dma_start(gate[:, first : first + (S - HEAD) // 3], wgo[:, first : first + (S - HEAD) // 3])
        w_raw = [[w_late[a], w_early[a][:]] for a in range(PASSES)]

        w_inter = [
            hold.tile([P, PASSES, P, 4], BF16, name=f"w_inter{m}", tag=f"turn{m}", align_bytes=4096) for m in range(M_TILES)
        ]
        w_codes = hold.tile([P, M_TILES, PASSES, P], U32, name="w_codes", align_bytes=256)
        w_scales = hold.tile([P, M_TILES, PASSES, P], U8, name="w_scales", align_bytes=256)
        warm = hold.tile([P, 8], F32, name="warm")
        nc.gpsimd.memset(warm[:, 0:1], 0.0)
        nc.scalar.activation(warm[:, 1:2], warm[:, 0:1], SILU)
        for m in (1, 0):
            for a in range(PASSES):
                nc.scalar.copy(
                    w_inter[m][:, a, :, :].rearrange("p (c i) j -> p c j i", i=4),
                    w_raw[a][m].rearrange("p j (c i) -> p c j i", i=4),
                )

        def quantise(m):
            nc.vector.quantize_mx(
                out=w_codes[:, m, :, :].rearrange("p a n -> p (a n)").bitcast(FP8X4),
                scales=w_scales[:, m, :, :].rearrange("p a n -> p (a n)"),
                in_=w_inter[m][:].rearrange("p a n j -> p (a n j)"),
            )

        def gather_last(first, last, tag):
            part = hold.tile([P, last - first], U32, name=f"picked_last{first}", tag=tag, align_bytes=256)
            nc.vector.tensor_copy(part[:], words[1][:].bitcast(U32).indirect(list_in[:, first // 16 : last // 16]))
            return part

        opening = shared.tile([P, HEAD], F32, name="opening", offset=2 * KIB, align_bytes=256)
        results = [hold.tile([P, S], F32, name=f"result{m}", align_bytes=256) for m in range(M_TILES)]

        def multiply(m, first, last, bank):
            acc = psum.tile([P, last - first], F32, name=f"acc{m}_{first}", tag=bank)
            for lo, hi in runs(first, last):
                part = 0 if lo < HEAD else 1
                rhs = [picked_first[:, lo:hi], picked_last[part][:, lo - HEAD * part : hi - HEAD * part]]
                for a in range(PASSES):
                    at = widths[part] * a - HEAD * part
                    nc.tensor.matmul_mx(
                        out=acc[:, lo - first : hi - first],
                        lhsT=w_codes[:, m, a, :].bitcast(FP8X4),
                        lhsT_scale=w_scales[:, m, a, :],
                        rhs=rhs[a].bitcast(FP8X4),
                        rhs_scale=planes[part][:, at + lo : at + hi],
                        start=(a == 0),
                        stop=(a == PASSES - 1),
                    )
            target = opening if (m == 1 and last <= HEAD) else results[m]
            nc.scalar.activation(target[:, first:last], acc[:], SILU, bias=bias[:, m : m + 1])

        def scatter(window, values, first, last):
            nc.vector.tensor_tensor(
                window[:].indirect(list_out[:, first // 16 : last // 16]), values, gate[:, first:last], MULT
            )

        picked_last = [gather_last(0, HEAD, "picked_early")]
        quantise(1)
        picked_last.append(gather_last(HEAD, S, "w_early1"))
        for i, (first, last) in enumerate(((0, 256), (256, 512), (512, 768), (768, HEAD))):
            multiply(1, first, last, f"bank1_{i}")
        quantise(0)
        window_second = hold.tile([P, T], F32, name="window_second", tag="turn0", align_bytes=4096)
        nc.gpsimd.memset(window_second[:], 0.0)
        for s in range(S // BANK):
            multiply(0, BANK * s, BANK * (s + 1), f"bank0_{s}")
        scatter(window_first, opening[:], 0, HEAD)
        multiply(1, HEAD, 2 * BANK, "bank1_0")
        for s in range(2, S // BANK):
            multiply(1, BANK * s, BANK * (s + 1), f"bank1_{s}")
        scatter(window_second, results[0][:], 0, S)
        nc.sync.dma_start(out[0:P, :], window_second[:])
        scatter(window_first, results[1][:, HEAD:S], HEAD, S)
        nc.sync.dma_start(out[P:M, :], window_first[:])
